import numpy as np
import ml_dtypes


def mxq(x, axis, fmt="e4m3"):
    dtype, down = {"e4m3": (ml_dtypes.float8_e4m3fn, 7), "e5m2": (ml_dtypes.float8_e5m2, 14)}[fmt]
    v = np.moveaxis(np.asarray(x, np.float32).astype(ml_dtypes.bfloat16).astype(np.float64), axis, -1)
    blocks = v.reshape(v.shape[:-1] + (-1, 32))
    amax = np.abs(blocks).max(-1, keepdims=True)
    byte = np.maximum(np.where(amax > 0, np.frexp(amax)[1] - 1 + 127, 0) - down, 1)
    scale = np.exp2(byte - 127.0)
    codes = (blocks / scale).astype(np.float32).astype(dtype).astype(np.float64)
    return np.moveaxis((codes * scale).reshape(v.shape), -1, axis)


WIDE = False


def mx_kscale(k):
    if not WIDE:
        return np.ones(k)
    levels = np.array([10, -10, 5, -5, 0])
    if k % 512:
        return np.exp2(np.random.permutation(np.resize(levels, k // 32))).repeat(32)
    a = np.empty((k // 512, 16))
    for p in range(k // 512):
        a[p, :8] = np.random.permutation(np.resize(levels, 8))
        for g in range(8):
            far = levels[np.abs(levels - a[p, g]) >= 10]
            a[p, g + 8] = far[np.random.randint(len(far))]
    return np.exp2(a.ravel()).repeat(32)


def f64(x):
    return np.asarray(x).astype(np.float64)


def striped(idx):
    return np.tile(np.asarray(idx).reshape(-1, 16).T, (8, 1)).astype(np.uint16)


def unstriped(offs):
    return offs[:16].T.reshape(-1).astype(np.int64)


E2M1 = np.array([0.0, 0.5, 1.0, 1.5, 2.0, 3.0, 4.0, 6.0, -0.0, -0.5, -1.0, -1.5, -2.0, -3.0, -4.0, -6.0])


def pack_weight(w, fmt):
    k, n = w.shape
    w = f64(np.asarray(w, np.float32).astype(ml_dtypes.bfloat16)).reshape(k // 32, 32, n)
    amax = np.abs(w).max(1)
    if fmt == "e4m3":
        byte = np.frexp(amax)[1] - 1 + 127 - 7
    else:
        mant, ex = np.frexp(amax / 6.0)
        byte = np.where(mant > 0.5, ex, ex - 1) + 127
    byte = np.clip(np.where(amax > 0, byte, 1), 1, 254)
    scaled = (w * np.exp2(127.0 - byte)[:, None, :]).reshape(k, n).astype(np.float32)
    by_word = np.ascontiguousarray(scaled.reshape(k // 512, 128, 4, n).transpose(0, 1, 3, 2))
    if fmt == "e4m3":
        words = by_word.astype(ml_dtypes.float8_e4m3fn).view(np.uint8)
    else:
        c = by_word.astype(ml_dtypes.float4_e2m1fn).view(np.uint8) & 0xF
        words = (c[..., 0::2] | (c[..., 1::2] << 4)).reshape(k // 512, 128, 2 * n)
    return np.ascontiguousarray(words), np.ascontiguousarray(byte.astype(np.uint8).reshape(k // 512, 16, n))


def unpack_weight(words, scales, fmt):
    g, _, n = scales.shape
    words = np.ascontiguousarray(words).reshape(g, 128, n, -1)
    if fmt == "e4m3":
        vals = words.view(ml_dtypes.float8_e4m3fn).astype(np.float64)
    else:
        nib = np.empty((g, 128, n, 4), np.uint8)
        nib[..., 0::2] = words & 0xF
        nib[..., 1::2] = words >> 4
        vals = E2M1[nib]
    vals = vals * np.repeat(np.exp2(scales.astype(np.float64) - 127.0), 8, axis=1)[..., None]
    return vals.transpose(0, 1, 3, 2).reshape(g * 512, n)


B, N, T, D, DV, NQ = 1, 2048, 4096, 1024, 128, 128
PAGE = 512


def setup_inputs():
    n = np.random.standard_normal
    pages = np.random.permutation(T // PAGE)[:B * N // PAGE]
    idx = (pages[:, None] * PAGE + np.arange(PAGE)[None, :]).reshape(-1)
    s = mx_kscale(D)[:, None]
    u = np.ones(T)
    u[idx] = mx_kscale(B * N)
    r = np.random.uniform(0.5, 2.0, T)
    qp = [pack_weight(x, "e4m3") for x in n((B, D, NQ)) * s * (0.80 / np.sqrt(D))]
    k = n((D, T)) / s
    v = n((DV, T)) / (u * r)
    kp = pack_weight(k, "e2m1")
    vp = pack_weight(v.T, "e4m3")
    return {
        "q_words": np.stack([x[0] for x in qp]),
        "q_scales": np.stack([x[1] for x in qp]),
        "k_words": np.ascontiguousarray(kp[0].reshape(D // 1024, 2, 128, T, 2).transpose(0, 2, 3, 1, 4)).reshape(D // 1024, 128, T, 4),
        "k_scales": kp[1],
        "v_words": vp[0],
        "v_scales": vp[1],
        "vs": np.tile(u * r, (128, 1)).astype(np.float32),
        "sink": (2.0 + 3.0 * n((B, NQ, 1))).astype(np.float32),
        "offs": striped(idx),
        "voffs": striped((pages[:, None] * DV + np.arange(DV)[None, :]).reshape(-1)),
    }


def reference(q_words, q_scales, k_words, k_scales, v_words, v_scales, vs, sink, offs, voffs):
    idx = unstriped(offs)
    k = unpack_weight(k_words.reshape(D // 1024, 128, T, 2, 2).transpose(0, 3, 1, 2, 4).reshape(D // 512, 128, 2 * T), k_scales, "e2m1")
    v = unpack_weight(v_words, v_scales, "e4m3")
    v = v.reshape(T // 512, 512, DV)[unstriped(voffs)[::DV] // DV].reshape(B, N, DV)
    pick = lambda x: x[:, idx].reshape(x.shape[0], B, N).transpose(1, 0, 2)
    q = np.stack([unpack_weight(q_words[b], q_scales[b], "e4m3") for b in range(B)])
    score = q.transpose(0, 2, 1) @ pick(k)
    m = np.maximum(score.max(-1, keepdims=True), f64(sink))
    p = np.exp(score - m)
    total = p.sum(-1, keepdims=True) + np.exp(f64(sink) - m)
    w = p * pick(f64(vs))[:, :1, :]
    y = mxq(w, 2, "e4m3") @ v
    y = y / total
    return y

@@ -1,0 +1,166 @@
+from contextlib import ExitStack
+
+import concourse.mybir as mybir
+from concourse.masks import make_identity
+
+N, T, D, DV, NQ = 2048, 4096, 1024, 128, 128
+P = 128
+PAGE = 512
+PAGES = N // PAGE
+POOL_PAGES = T // PAGE
+PASSES = D // 512
+
+FLOPS = 2 * NQ * N * (D + DV)
+
+F32 = mybir.dt.float32
+BF16 = mybir.dt.bfloat16
+I32 = mybir.dt.int32
+U32 = mybir.dt.uint32
+U16 = mybir.dt.uint16
+U8 = mybir.dt.uint8
+FP8X4 = mybir.dt.float8_e4m3fn_x4
+FP4X4 = mybir.dt.float4_e2m1fn_x4
+ALU = mybir.AluOpType
+ACT = mybir.ActivationFunctionType
+AX = mybir.AxisListType
+
+
+def tile_attend_pkv4q_soft_sink_kernel(
+    tc, q_words, q_scales, k_words, k_scales, v_words, v_scales, vs, sink, offs, voffs, out
+):
+    nc = tc.nc
+    with ExitStack() as ctx:
+        lists = ctx.enter_context(tc.tile_pool(name="lists", bufs=1))
+        keep = ctx.enter_context(tc.tile_pool(name="keep", bufs=1))
+        shared = ctx.enter_context(tc.tile_pool(name="shared", bufs=1))
+        psum = ctx.enter_context(tc.psum_pool(name="psum", bufs=1))
+        turn = ctx.enter_context(tc.psum_pool(name="turn", bufs=3))
+
+        key_list = lists.tile([P, N // 16], U16, name="key_list")
+        value_list = lists.tile([P, PAGES * DV // 16], U16, name="value_list")
+        nc.sync.dma_start(key_list[:], offs)
+
+        key_pool = keep.tile([P, T], I32, name="key_pool", align_bytes=64)
+        nc.sync.dma_start(key_pool[:], k_words[0].rearrange("p t b -> p (t b)").bitcast(I32))
+
+        key_scale_pool = shared.tile([P, T], U8, name="key_scale_pool", offset=15360)
+        nc.vector.memset(key_scale_pool[:].bitcast(I32), 0)
+        nc.scalar.dma_start(
+            key_scale_pool[:].bitcast(I32)[0:P:4, :],
+            k_scales.rearrange("o f t -> (o f) t").bitcast(I32),
+        )
+
+        q_codes = keep.tile([P, PASSES, NQ], I32, name="q_codes", align_bytes=64)
+        nc.sync.dma_start(q_codes[:], q_words[0].rearrange("o p q r -> p o (q r)").bitcast(I32))
+        nc.sync.dma_start(value_list[:], voffs)
+
+        sink_col = keep.tile([P, 1], F32, name="sink_col")
+        nc.gpsimd.dma_start(sink_col[:], sink[0])
+        q_plane = keep.tile([P, PASSES, NQ], U8, name="q_plane", align_bytes=64)
+        nc.gpsimd.memset(q_plane[:].bitcast(I32), 0)
+        q_rows = q_scales[0].bitcast(I32).rearrange("o f q -> f o q")
+        for j in range(4):
+            nc.gpsimd.dma_start(q_plane[:].bitcast(I32)[j:P:32, :, :], q_rows[j:16:4, :, :])
+        ident = keep.tile([P, P], F32, name="ident")
+        make_identity(nc, ident[:])
+
+        warm = keep.tile([P, 1], F32, name="warm")
+        nc.scalar.activation(warm[:], sink_col[:], ACT.Exp, scale=0.0)
+
+        key_planes = [keep.tile([P, N], U8, name=f"key_plane{o}", align_bytes=64) for o in range(PASSES)]
+        for o in range(PASSES):
+            nc.vector.memset(key_planes[o][:].bitcast(I32), 0)
+
+        key_scales_listed = keep.tile([P, N], U8, name="key_scales_listed")
+        nc.vector.tensor_copy(key_scales_listed[:], key_scale_pool[:].indirect(key_list[:]))
+        for o in range(PASSES):
+            for j in range(4):
+                nc.sync.dma_start(
+                    key_planes[o][:].bitcast(I32)[j:P:32, :],
+                    key_scales_listed[:].bitcast(I32)[64 * o + 4 * j : 64 * (o + 1) : 16, :],
+                )
+
+        value_pool = shared.tile([P, POOL_PAGES, DV], I32, name="value_pool", offset=17408)
+        nc.sync.dma_start(value_pool[:], v_words.rearrange("u p e r -> p u (e r)").bitcast(I32))
+        value_scale_pool = shared.tile([P, POOL_PAGES, DV], U8, name="value_scale_pool", offset=16384)
+        nc.vector.memset(value_scale_pool[:].bitcast(I32), 0)
+        v_rows = v_scales.bitcast(I32).rearrange("u f e -> f u e")
+        for j in range(4):
+            nc.sync.dma_start(value_scale_pool[:].bitcast(I32)[j:P:32, :, :], v_rows[j:16:4, :, :])
+        token_scale_pool = shared.tile([P, T], F32, name="token_scale_pool", offset=0)
+        nc.sync.dma_start(token_scale_pool[:], vs)
+
+        neg_max = keep.tile([P, 1], F32, name="neg_sink")
+        nc.vector.tensor_scalar(neg_max[:], sink_col[:], -1.0, None, ALU.mult)
+
+        neg_scores = []
+        for c in range(PAGES):
+            page_list = key_list[:, c * PAGE // 16 : (c + 1) * PAGE // 16]
+            key_pairs = keep.tile([P, PAGE], U32, name=f"key_pairs{c}")
+            nc.vector.tensor_copy(key_pairs[:], key_pool[:].bitcast(U32).indirect(page_list))
+            key_codes = keep.tile([P, PASSES, PAGE], U16, name=f"key_codes{c}", align_bytes=64)
+            nc.vector.tensor_copy(key_codes[:], key_pairs[:].bitcast(U16).rearrange("p (n o) -> p o n", o=PASSES))
+            scores = psum.tile([P, PAGE], F32, name=f"scores{c}")
+            for o in range(PASSES):
+                nc.tensor.matmul_mx(
+                    out=scores[:],
+                    lhsT=q_codes[:, o, :].bitcast(FP8X4),
+                    lhsT_scale=q_plane[:, o, :],
+                    rhs=key_codes[:, o, :].bitcast(FP4X4),
+                    rhs_scale=key_planes[o][:, c * PAGE : (c + 1) * PAGE],
+                    start=(o == 0),
+                    stop=(o == PASSES - 1),
+                )
+            negated = keep.tile([P, PAGE], F32, name=f"negated{c}")
+            running = keep.tile([P, 1], F32, name=f"neg_max{c}")
+            nc.vector.tensor_scalar(negated[:], scores[:], -1.0, neg_max[:], ALU.mult, ALU.min, accum_out=running[:])
+            neg_max = running
+            neg_scores.append(negated)
+
+        value_codes = keep.tile([P, PAGES * DV], U32, name="value_codes", align_bytes=64)
+        nc.vector.tensor_copy(
+            value_codes[:], value_pool[:].rearrange("p u e -> p (u e)").bitcast(U32).indirect(value_list[:])
+        )
+        value_plane = keep.tile([P, PAGES * DV], U8, name="value_plane", align_bytes=64)
+        nc.vector.tensor_copy(
+            value_plane[:], value_scale_pool[:].rearrange("p u e -> p (u e)").indirect(value_list[:])
+        )
+
+        sums = keep.tile([P, PAGES + 1], F32, name="sums")
+        acc = psum.tile([P, DV], F32, name="acc")
+        for c in range(PAGES):
+            page_list = key_list[:, c * PAGE // 16 : (c + 1) * PAGE // 16]
+            probs = keep.tile([P, PAGE], F32, name=f"probs{c}")
+            nc.scalar.activation(
+                probs[:], neg_scores[c][:], ACT.Exp, bias=neg_max[:], scale=-1.0, accum_out=sums[:, c : c + 1]
+            )
+            weights = keep.tile([P, PAGE], F32, name=f"weights{c}")
+            nc.vector.tensor_tensor(weights[:], token_scale_pool[:].indirect(page_list), probs[:], ALU.mult)
+            turned = turn.tile([P, 4, NQ], F32, name="turned")
+            for t in range(4):
+                nc.tensor.transpose(turned[:, t, :], weights[:, t:PAGE:4], ident[:])
+            grouped = keep.tile([P, NQ, 4], BF16, name=f"grouped{c}", align_bytes=64)
+            nc.scalar.copy(grouped[:], turned[:].rearrange("p t q -> p q t"))
+            w_codes = keep.tile([P, NQ], U32, name=f"w_codes{c}", align_bytes=64)
+            w_plane = keep.tile([P, NQ], U8, name=f"w_plane{c}", align_bytes=64)
+            nc.vector.quantize_mx(
+                out=w_codes[:].bitcast(FP8X4), scales=w_plane[:], in_=grouped[:].rearrange("p q t -> p (q t)")
+            )
+            nc.tensor.matmul_mx(
+                out=acc[:],
+                lhsT=w_codes[:].bitcast(FP8X4),
+                lhsT_scale=w_plane[:],
+                rhs=value_codes[:, c * DV : (c + 1) * DV].bitcast(FP8X4),
+                rhs_scale=value_plane[:, c * DV : (c + 1) * DV],
+                start=(c == 0),
+                stop=(c == PAGES - 1),
+            )
+
+        nc.scalar.activation(sums[:, PAGES : PAGES + 1], sink_col[:], ACT.Exp, bias=neg_max[:])
+        total = keep.tile([P, 1], F32, name="total")
+        nc.vector.tensor_reduce(total[:], sums[:], AX.X, ALU.add)
+        inverse = keep.tile([P, 1], F32, name="inverse")
+        nc.vector.reciprocal(inverse[:], total[:])
+        result = keep.tile([P, DV], F32, name="result")
+        nc.vector.tensor_scalar(result[:], acc[:], inverse[:], None, ALU.mult)
+        nc.sync.dma_start(out[0], result[:])

@@ -34,7 +34,6 @@ def tile_attend_pkv4q_soft_sink_kernel(
         keep = ctx.enter_context(tc.tile_pool(name="keep", bufs=1))
         shared = ctx.enter_context(tc.tile_pool(name="shared", bufs=1))
         psum = ctx.enter_context(tc.psum_pool(name="psum", bufs=1))
-        turn = ctx.enter_context(tc.psum_pool(name="turn", bufs=3))
 
         key_list = lists.tile([P, N // 16], U16, name="key_list")
         value_list = lists.tile([P, PAGES * DV // 16], U16, name="value_list")
@@ -43,10 +42,11 @@ def tile_attend_pkv4q_soft_sink_kernel(
         key_pool = keep.tile([P, T], I32, name="key_pool", align_bytes=64)
         nc.sync.dma_start(key_pool[:], k_words[0].rearrange("p t b -> p (t b)").bitcast(I32))
 
-        key_scale_pool = shared.tile([P, T], U8, name="key_scale_pool", offset=15360)
-        nc.vector.memset(key_scale_pool[:].bitcast(I32), 0)
+        key_scale_room = shared.tile([P, 6144], U8, name="key_scale_room", offset=16352)
+        key_scale_pool = key_scale_room[:, 0:T]
+        nc.vector.memset(key_scale_pool.bitcast(I32), 0)
         nc.scalar.dma_start(
-            key_scale_pool[:].bitcast(I32)[0:P:4, :],
+            key_scale_pool.bitcast(I32)[0:P:4, :],
             k_scales.rearrange("o f t -> (o f) t").bitcast(I32),
         )
 
@@ -60,7 +60,7 @@ def tile_attend_pkv4q_soft_sink_kernel(
         nc.gpsimd.memset(q_plane[:].bitcast(I32), 0)
         q_rows = q_scales[0].bitcast(I32).rearrange("o f q -> f o q")
         for j in range(4):
-            nc.gpsimd.dma_start(q_plane[:].bitcast(I32)[j:P:32, :, :], q_rows[j:16:4, :, :])
+            nc.gpsimd.dma_start(q_plane[:].bitcast(I32)[32 * j : 32 * j + 4, :, :], q_rows[4 * j : 4 * j + 4, :, :])
         ident = keep.tile([P, P], F32, name="ident")
         make_identity(nc, ident[:])
 
@@ -72,12 +72,12 @@ def tile_attend_pkv4q_soft_sink_kernel(
             nc.vector.memset(key_planes[o][:].bitcast(I32), 0)
 
         key_scales_listed = keep.tile([P, N], U8, name="key_scales_listed")
-        nc.vector.tensor_copy(key_scales_listed[:], key_scale_pool[:].indirect(key_list[:]))
+        nc.vector.tensor_copy(key_scales_listed[:], key_scale_pool.indirect(key_list[:]))
         for o in range(PASSES):
             for j in range(4):
                 nc.sync.dma_start(
-                    key_planes[o][:].bitcast(I32)[j:P:32, :],
-                    key_scales_listed[:].bitcast(I32)[64 * o + 4 * j : 64 * (o + 1) : 16, :],
+                    key_planes[o][:].bitcast(I32)[32 * j : 32 * j + 4, :],
+                    key_scales_listed[:].bitcast(I32)[64 * o + 16 * j : 64 * o + 16 * (j + 1) : 4, :],
                 )
 
         value_pool = shared.tile([P, POOL_PAGES, DV], I32, name="value_pool", offset=17408)
@@ -86,21 +86,22 @@ def tile_attend_pkv4q_soft_sink_kernel(
         nc.vector.memset(value_scale_pool[:].bitcast(I32), 0)
         v_rows = v_scales.bitcast(I32).rearrange("u f e -> f u e")
         for j in range(4):
-            nc.sync.dma_start(value_scale_pool[:].bitcast(I32)[j:P:32, :, :], v_rows[j:16:4, :, :])
+            nc.sync.dma_start(value_scale_pool[:].bitcast(I32)[32 * j : 32 * j + 4, :, :], v_rows[4 * j : 4 * j + 4, :, :])
         token_scale_pool = shared.tile([P, T], F32, name="token_scale_pool", offset=0)
         nc.sync.dma_start(token_scale_pool[:], vs)
 
         neg_max = keep.tile([P, 1], F32, name="neg_sink")
         nc.vector.tensor_scalar(neg_max[:], sink_col[:], -1.0, None, ALU.mult)
 
+        key_pairs = shared.tile([P, N], U32, name="key_pairs", offset=21504)
         neg_scores = []
         for c in range(PAGES):
             page_list = key_list[:, c * PAGE // 16 : (c + 1) * PAGE // 16]
-            key_pairs = keep.tile([P, PAGE], U32, name=f"key_pairs{c}")
-            nc.vector.tensor_copy(key_pairs[:], key_pool[:].bitcast(U32).indirect(page_list))
+            page_pairs = key_pairs[:, c * PAGE : (c + 1) * PAGE]
+            nc.vector.tensor_copy(page_pairs, key_pool[:].bitcast(U32).indirect(page_list))
             key_codes = keep.tile([P, PASSES, PAGE], U16, name=f"key_codes{c}", align_bytes=64)
-            nc.vector.tensor_copy(key_codes[:], key_pairs[:].bitcast(U16).rearrange("p (n o) -> p o n", o=PASSES))
-            scores = psum.tile([P, PAGE], F32, name=f"scores{c}")
+            nc.vector.tensor_copy(key_codes[:], page_pairs.bitcast(U16).rearrange("p (n o) -> p o n", o=PASSES))
+            scores = psum.tile([P, PAGE], F32, name=f"scores{c}", tag=f"scores{c}")
             for o in range(PASSES):
                 nc.tensor.matmul_mx(
                     out=scores[:],
@@ -127,24 +128,47 @@ def tile_attend_pkv4q_soft_sink_kernel(
         )
 
         sums = keep.tile([P, PAGES + 1], F32, name="sums")
-        acc = psum.tile([P, DV], F32, name="acc")
+        probs = keep.tile([P, PAGES, PAGE], F32, name="probs")
+        for c in range(PAGES):
+            nc.scalar.activation(
+                probs[:, c, :], neg_scores[c][:], ACT.Exp, bias=neg_max[:], scale=-1.0, accum_out=sums[:, c : c + 1]
+            )
+        nc.scalar.activation(sums[:, PAGES : PAGES + 1], sink_col[:], ACT.Exp, bias=neg_max[:])
+
+        weights = keep.tile([P, PAGES, PAGE], F32, name="weights")
         for c in range(PAGES):
             page_list = key_list[:, c * PAGE // 16 : (c + 1) * PAGE // 16]
-            probs = keep.tile([P, PAGE], F32, name=f"probs{c}")
-            nc.scalar.activation(
-                probs[:], neg_scores[c][:], ACT.Exp, bias=neg_max[:], scale=-1.0, accum_out=sums[:, c : c + 1]
-            )
-            weights = keep.tile([P, PAGE], F32, name=f"weights{c}")
-            nc.vector.tensor_tensor(weights[:], token_scale_pool[:].indirect(page_list), probs[:], ALU.mult)
-            turned = turn.tile([P, 4, NQ], F32, name="turned")
-            for t in range(4):
-                nc.tensor.transpose(turned[:, t, :], weights[:, t:PAGE:4], ident[:])
-            grouped = keep.tile([P, NQ, 4], BF16, name=f"grouped{c}", align_bytes=64)
-            nc.scalar.copy(grouped[:], turned[:].rearrange("p t q -> p q t"))
+            nc.vector.tensor_tensor(weights[:, c, :], token_scale_pool[:].indirect(page_list), probs[:, c, :], ALU.mult)
+
+        rounded = keep.tile([P, PAGES, 2, P, 2], BF16, name="rounded")
+        for c in range(PAGES):
+            by_word = weights[:, c, :].rearrange("q (s u e) -> q u s e", u=2, e=2)
+            if c == 0:
+                nc.scalar.copy(rounded[:, c, :, :, :], by_word)
+            else:
+                nc.vector.tensor_copy(rounded[:, c, :, :, :], by_word)
+
+        total = keep.tile([P, 1], F32, name="total")
+        nc.vector.tensor_reduce(total[:], sums[:], AX.X, ALU.add)
+        inverse = keep.tile([P, 1], F32, name="inverse")
+        nc.vector.reciprocal(inverse[:], total[:])
+
+        grouped = keep.tile([P, PAGES, NQ, 4], BF16, name="grouped", align_bytes=64)
+        for c in range(PAGES):
+            turned = psum.tile([P, 2, NQ], F32, name=f"turned{c}")
+            for u in range(2):
+                words = rounded[:, c, u, :, :].rearrange("q s e -> q (s e)").bitcast(F32)
+                nc.tensor.transpose(turned[:, u, :], words, ident[:])
+            nc.scalar.copy(grouped[:, c, :, :].bitcast(F32), turned[:].rearrange("s u q -> s q u"))
+
+        acc = psum.tile([P, DV], F32, name="acc", tag="scores0")
+        for c in range(PAGES):
             w_codes = keep.tile([P, NQ], U32, name=f"w_codes{c}", align_bytes=64)
             w_plane = keep.tile([P, NQ], U8, name=f"w_plane{c}", align_bytes=64)
             nc.vector.quantize_mx(
-                out=w_codes[:].bitcast(FP8X4), scales=w_plane[:], in_=grouped[:].rearrange("p q t -> p (q t)")
+                out=w_codes[:].bitcast(FP8X4),
+                scales=w_plane[:],
+                in_=grouped[:, c, :, :].rearrange("p q t -> p (q t)"),
             )
             nc.tensor.matmul_mx(
                 out=acc[:],
@@ -156,11 +180,6 @@ def tile_attend_pkv4q_soft_sink_kernel(
                 stop=(c == PAGES - 1),
             )
 
-        nc.scalar.activation(sums[:, PAGES : PAGES + 1], sink_col[:], ACT.Exp, bias=neg_max[:])
-        total = keep.tile([P, 1], F32, name="total")
-        nc.vector.tensor_reduce(total[:], sums[:], AX.X, ALU.add)
-        inverse = keep.tile([P, 1], F32, name="inverse")
-        nc.vector.reciprocal(inverse[:], total[:])
         result = keep.tile([P, DV], F32, name="result")
         nc.vector.tensor_scalar(result[:], acc[:], inverse[:], None, ALU.mult)
         nc.sync.dma_start(out[0], result[:])

@@ -40,9 +40,13 @@ def tile_attend_pkv4q_soft_sink_kernel(
         nc.sync.dma_start(key_list[:], offs)
 
         key_pool = keep.tile([P, T], I32, name="key_pool", align_bytes=64)
-        nc.sync.dma_start(key_pool[:], k_words[0].rearrange("p t b -> p (t b)").bitcast(I32))
+        nc.gpsimd.dma_start(key_pool[:], k_words[0].rearrange("p t b -> p (t b)").bitcast(I32))
+        value_pool = keep.tile([P, POOL_PAGES, DV], I32, name="value_pool")
+        nc.gpsimd.dma_start(value_pool[:], v_words.rearrange("u p e r -> p u (e r)").bitcast(I32))
+        token_scale_pool = keep.tile([P, T], F32, name="token_scale_pool")
+        nc.gpsimd.dma_start(token_scale_pool[:], vs)
 
-        key_scale_room = shared.tile([P, 6144], U8, name="key_scale_room", offset=16352)
+        key_scale_room = shared.tile([P, T], U8, name="key_scale_room", offset=0)
         key_scale_pool = key_scale_room[:, 0:T]
         nc.vector.memset(key_scale_pool.bitcast(I32), 0)
         nc.scalar.dma_start(
@@ -55,12 +59,12 @@ def tile_attend_pkv4q_soft_sink_kernel(
         nc.sync.dma_start(value_list[:], voffs)
 
         sink_col = keep.tile([P, 1], F32, name="sink_col")
-        nc.gpsimd.dma_start(sink_col[:], sink[0])
+        nc.sync.dma_start(sink_col[:], sink[0])
         q_plane = keep.tile([P, PASSES, NQ], U8, name="q_plane", align_bytes=64)
-        nc.gpsimd.memset(q_plane[:].bitcast(I32), 0)
+        nc.vector.memset(q_plane[:].bitcast(I32), 0)
         q_rows = q_scales[0].bitcast(I32).rearrange("o f q -> f o q")
         for j in range(4):
-            nc.gpsimd.dma_start(q_plane[:].bitcast(I32)[32 * j : 32 * j + 4, :, :], q_rows[4 * j : 4 * j + 4, :, :])
+            nc.sync.dma_start(q_plane[:].bitcast(I32)[32 * j : 32 * j + 4, :, :], q_rows[4 * j : 4 * j + 4, :, :])
         ident = keep.tile([P, P], F32, name="ident")
         make_identity(nc, ident[:])
 
@@ -80,20 +84,16 @@ def tile_attend_pkv4q_soft_sink_kernel(
                     key_scales_listed[:].bitcast(I32)[64 * o + 16 * j : 64 * o + 16 * (j + 1) : 4, :],
                 )
 
-        value_pool = shared.tile([P, POOL_PAGES, DV], I32, name="value_pool", offset=17408)
-        nc.sync.dma_start(value_pool[:], v_words.rearrange("u p e r -> p u (e r)").bitcast(I32))
-        value_scale_pool = shared.tile([P, POOL_PAGES, DV], U8, name="value_scale_pool", offset=16384)
+        value_scale_pool = shared.tile([P, POOL_PAGES, DV], U8, name="value_scale_pool", offset=0)
         nc.vector.memset(value_scale_pool[:].bitcast(I32), 0)
         v_rows = v_scales.bitcast(I32).rearrange("u f e -> f u e")
         for j in range(4):
             nc.sync.dma_start(value_scale_pool[:].bitcast(I32)[32 * j : 32 * j + 4, :, :], v_rows[4 * j : 4 * j + 4, :, :])
-        token_scale_pool = shared.tile([P, T], F32, name="token_scale_pool", offset=0)
-        nc.sync.dma_start(token_scale_pool[:], vs)
 
         neg_max = keep.tile([P, 1], F32, name="neg_sink")
         nc.vector.tensor_scalar(neg_max[:], sink_col[:], -1.0, None, ALU.mult)
 
-        key_pairs = shared.tile([P, N], U32, name="key_pairs", offset=21504)
+        key_pairs = shared.tile([P, N], U32, name="key_pairs", offset=1024)
         neg_scores = []
         for c in range(PAGES):
             page_list = key_list[:, c * PAGE // 16 : (c + 1) * PAGE // 16]

@@ -43,10 +43,8 @@ def tile_attend_pkv4q_soft_sink_kernel(
         nc.gpsimd.dma_start(key_pool[:], k_words[0].rearrange("p t b -> p (t b)").bitcast(I32))
         value_pool = keep.tile([P, POOL_PAGES, DV], I32, name="value_pool")
         nc.gpsimd.dma_start(value_pool[:], v_words.rearrange("u p e r -> p u (e r)").bitcast(I32))
-        token_scale_pool = keep.tile([P, T], F32, name="token_scale_pool")
-        nc.gpsimd.dma_start(token_scale_pool[:], vs)
 
-        key_scale_room = shared.tile([P, T], U8, name="key_scale_room", offset=0)
+        key_scale_room = shared.tile([P, 9216], U8, name="key_scale_room", offset=16352)
         key_scale_pool = key_scale_room[:, 0:T]
         nc.vector.memset(key_scale_pool.bitcast(I32), 0)
         nc.scalar.dma_start(
@@ -84,20 +82,22 @@ def tile_attend_pkv4q_soft_sink_kernel(
                     key_scales_listed[:].bitcast(I32)[64 * o + 16 * j : 64 * o + 16 * (j + 1) : 4, :],
                 )
 
-        value_scale_pool = shared.tile([P, POOL_PAGES, DV], U8, name="value_scale_pool", offset=0)
+        value_scale_pool = shared.tile([P, POOL_PAGES, DV], U8, name="value_scale_pool", offset=16384)
         nc.vector.memset(value_scale_pool[:].bitcast(I32), 0)
         v_rows = v_scales.bitcast(I32).rearrange("u f e -> f u e")
         for j in range(4):
             nc.sync.dma_start(value_scale_pool[:].bitcast(I32)[32 * j : 32 * j + 4, :, :], v_rows[4 * j : 4 * j + 4, :, :])
+        token_scale_pool = shared.tile([P, T], F32, name="token_scale_pool", offset=0)
+        nc.sync.dma_start(token_scale_pool[:], vs)
 
-        neg_max = keep.tile([P, 1], F32, name="neg_sink")
-        nc.vector.tensor_scalar(neg_max[:], sink_col[:], -1.0, None, ALU.mult)
+        neg_maxima = shared.tile([P, PAGES + 1], F32, name="neg_maxima", offset=25600)
+        nc.vector.tensor_scalar(neg_maxima[:, PAGES:], sink_col[:], -1.0, None, ALU.mult)
 
-        key_pairs = shared.tile([P, N], U32, name="key_pairs", offset=1024)
         neg_scores = []
         for c in range(PAGES):
             page_list = key_list[:, c * PAGE // 16 : (c + 1) * PAGE // 16]
-            page_pairs = key_pairs[:, c * PAGE : (c + 1) * PAGE]
+            key_pairs = shared.tile([P, PAGE], U32, name=f"key_pairs{c}", offset=17408 + 2048 * c)
+            page_pairs = key_pairs[:]
             nc.vector.tensor_copy(page_pairs, key_pool[:].bitcast(U32).indirect(page_list))
             key_codes = keep.tile([P, PASSES, PAGE], U16, name=f"key_codes{c}", align_bytes=64)
             nc.vector.tensor_copy(key_codes[:], page_pairs.bitcast(U16).rearrange("p (n o) -> p o n", o=PASSES))
@@ -113,53 +113,76 @@ def tile_attend_pkv4q_soft_sink_kernel(
                     stop=(o == PASSES - 1),
                 )
             negated = keep.tile([P, PAGE], F32, name=f"negated{c}")
-            running = keep.tile([P, 1], F32, name=f"neg_max{c}")
-            nc.vector.tensor_scalar(negated[:], scores[:], -1.0, neg_max[:], ALU.mult, ALU.min, accum_out=running[:])
-            neg_max = running
+            nc.vector.tensor_scalar(
+                negated[:], scores[:], -1.0, None, ALU.mult, ALU.min, accum_out=neg_maxima[:, c : c + 1]
+            )
             neg_scores.append(negated)
+        neg_max = keep.tile([P, 1], F32, name="neg_max")
+        nc.vector.tensor_reduce(neg_max[:], neg_maxima[:], AX.X, ALU.min)
 
         value_codes = keep.tile([P, PAGES * DV], U32, name="value_codes", align_bytes=64)
         nc.vector.tensor_copy(
             value_codes[:], value_pool[:].rearrange("p u e -> p (u e)").bitcast(U32).indirect(value_list[:])
         )
-        value_plane = keep.tile([P, PAGES * DV], U8, name="value_plane", align_bytes=64)
-        nc.vector.tensor_copy(
-            value_plane[:], value_scale_pool[:].rearrange("p u e -> p (u e)").indirect(value_list[:])
-        )
+        value_scale_window = value_scale_pool[:].rearrange("p u e -> p (u e)")
+        early_plane = shared.tile([P, 2 * DV], U8, name="early_plane", align_bytes=64, offset=25600)
+        nc.vector.tensor_copy(early_plane[:], value_scale_window.indirect(value_list[:, 0:16]))
 
-        sums = keep.tile([P, PAGES + 1], F32, name="sums")
-        probs = keep.tile([P, PAGES, PAGE], F32, name="probs")
-        for c in range(PAGES):
+        exp_cuts = [0, 256, 512, 1024, 1536, 2048]
+        sums = keep.tile([P, len(exp_cuts)], F32, name="sums")
+        probs = {}
+        for i, (lo, hi) in enumerate(zip(exp_cuts, exp_cuts[1:])):
+            c = lo // PAGE
+            probs[lo] = keep.tile([P, hi - lo], F32, name=f"probs{lo}")
             nc.scalar.activation(
-                probs[:, c, :], neg_scores[c][:], ACT.Exp, bias=neg_max[:], scale=-1.0, accum_out=sums[:, c : c + 1]
+                probs[lo][:],
+                neg_scores[c][:, lo - c * PAGE : hi - c * PAGE],
+                ACT.Exp,
+                bias=neg_max[:],
+                scale=-1.0,
+                accum_out=sums[:, i : i + 1],
             )
-        nc.scalar.activation(sums[:, PAGES : PAGES + 1], sink_col[:], ACT.Exp, bias=neg_max[:])
 
-        weights = keep.tile([P, PAGES, PAGE], F32, name="weights")
+        cuts = [0, 256, 512, 1024, 1536, 1920, 2048]
+        weights = {}
+        for lo, hi in zip(cuts, cuts[1:]):
+            start = max(e for e in exp_cuts if e <= lo)
+            weights[lo] = keep.tile([P, hi - lo], F32, name=f"weights{lo}")
+            nc.vector.tensor_tensor(
+                weights[lo][:],
+                token_scale_pool[:].indirect(key_list[:, lo // 16 : hi // 16]),
+                probs[start][:, lo - start : hi - start],
+                ALU.mult,
+            )
+
+        grouped = []
         for c in range(PAGES):
-            page_list = key_list[:, c * PAGE // 16 : (c + 1) * PAGE // 16]
-            nc.vector.tensor_tensor(weights[:, c, :], token_scale_pool[:].indirect(page_list), probs[:, c, :], ALU.mult)
-
-        rounded = keep.tile([P, PAGES, 2, P, 2], BF16, name="rounded")
-        for c in range(PAGES):
-            by_word = weights[:, c, :].rearrange("q (s u e) -> q u s e", u=2, e=2)
-            if c == 0:
-                nc.scalar.copy(rounded[:, c, :, :, :], by_word)
-            else:
-                nc.vector.tensor_copy(rounded[:, c, :, :, :], by_word)
-
-        total = keep.tile([P, 1], F32, name="total")
-        nc.vector.tensor_reduce(total[:], sums[:], AX.X, ALU.add)
-        inverse = keep.tile([P, 1], F32, name="inverse")
-        nc.vector.reciprocal(inverse[:], total[:])
-
-        grouped = keep.tile([P, PAGES, NQ, 4], BF16, name="grouped", align_bytes=64)
-        for c in range(PAGES):
+            rounded = keep.tile([P, 2, P, 2], BF16, name=f"rounded{c}")
+            for lo, hi in zip(cuts, cuts[1:]):
+                if lo // PAGE == c:
+                    by_word = weights[lo][:].rearrange("q (s u e) -> q u s e", u=2, e=2)
+                    into = rounded[:, :, (lo - c * PAGE) // 4 : (hi - c * PAGE) // 4, :]
+                    if c < PAGES - 1:
+                        nc.scalar.copy(into, by_word)
+                    else:
+                        nc.vector.tensor_copy(into, by_word)
             turned = psum.tile([P, 2, NQ], F32, name=f"turned{c}")
             for u in range(2):
-                words = rounded[:, c, u, :, :].rearrange("q s e -> q (s e)").bitcast(F32)
+                words = rounded[:, u, :, :].rearrange("q s e -> q (s e)").bitcast(F32)
                 nc.tensor.transpose(turned[:, u, :], words, ident[:])
-            nc.scalar.copy(grouped[:, c, :, :].bitcast(F32), turned[:].rearrange("s u q -> s q u"))
+            grouped.append(keep.tile([P, NQ, 4], BF16, name=f"grouped{c}", align_bytes=64))
+            nc.scalar.copy(grouped[c][:].bitcast(F32), turned[:].rearrange("s u q -> s q u"))
+
+        nc.scalar.activation(sums[:, len(exp_cuts) - 1 :], sink_col[:], ACT.Exp, bias=neg_max[:])
+        total = keep.tile([P, 1], F32, name="total")
+        sums_again = keep.tile([P, len(exp_cuts)], F32, name="sums_again")
+        nc.scalar.activation(sums_again[:], sums[:], ACT.Copy, accum_out=total[:])
+
+        late_plane = shared.tile([P, 2 * DV], U8, name="late_plane", align_bytes=64, offset=64)
+        nc.vector.tensor_copy(late_plane[:], value_scale_window.indirect(value_list[:, 16:32]))
+        value_planes = [early_plane, late_plane]
+        inverse = shared.tile([P, 1], F32, name="inverse", offset=0)
+        nc.vector.reciprocal(inverse[:], total[:])
 
         acc = psum.tile([P, DV], F32, name="acc", tag="scores0")
         for c in range(PAGES):
@@ -168,14 +191,14 @@ def tile_attend_pkv4q_soft_sink_kernel(
             nc.vector.quantize_mx(
                 out=w_codes[:].bitcast(FP8X4),
                 scales=w_plane[:],
-                in_=grouped[:, c, :, :].rearrange("p q t -> p (q t)"),
+                in_=grouped[c][:].rearrange("p q t -> p (q t)"),
             )
             nc.tensor.matmul_mx(
                 out=acc[:],
                 lhsT=w_codes[:].bitcast(FP8X4),
                 lhsT_scale=w_plane[:],
                 rhs=value_codes[:, c * DV : (c + 1) * DV].bitcast(FP8X4),
-                rhs_scale=value_plane[:, c * DV : (c + 1) * DV],
+                rhs_scale=value_planes[c // 2][:, c % 2 * DV : (c % 2 + 1) * DV],
                 start=(c == 0),
                 stop=(c == PAGES - 1),
             )

@@ -39,149 +39,148 @@ def tile_attend_pkv4q_soft_sink_kernel(
         value_list = lists.tile([P, PAGES * DV // 16], U16, name="value_list")
         nc.sync.dma_start(key_list[:], offs)
 
-        key_pool = keep.tile([P, T], I32, name="key_pool", align_bytes=64)
-        nc.gpsimd.dma_start(key_pool[:], k_words[0].rearrange("p t b -> p (t b)").bitcast(I32))
-        value_pool = keep.tile([P, POOL_PAGES, DV], I32, name="value_pool")
-        nc.gpsimd.dma_start(value_pool[:], v_words.rearrange("u p e r -> p u (e r)").bitcast(I32))
-
-        key_scale_room = shared.tile([P, 9216], U8, name="key_scale_room", offset=16352)
+        key_scale_room = shared.tile([P, T + 64], U8, name="key_scale_room", align_bytes=64, offset=0)
         key_scale_pool = key_scale_room[:, 0:T]
-        nc.vector.memset(key_scale_pool.bitcast(I32), 0)
-        nc.scalar.dma_start(
-            key_scale_pool.bitcast(I32)[0:P:4, :],
+        nc.sync.dma_start(
+            key_scale_pool.bitcast(I32)[0:32, :],
             k_scales.rearrange("o f t -> (o f) t").bitcast(I32),
         )
+        nc.vector.memset(key_scale_pool.bitcast(I32)[32:64, :], 0)
+        nc.vector.memset(key_scale_pool.bitcast(I32)[64:128, :], 0)
 
-        q_codes = keep.tile([P, PASSES, NQ], I32, name="q_codes", align_bytes=64)
-        nc.sync.dma_start(q_codes[:], q_words[0].rearrange("o p q r -> p o (q r)").bitcast(I32))
+        key_pool = keep.tile([P, T], I32, name="key_pool", align_bytes=64)
+        nc.sync.dma_start(key_pool[:], k_words[0].rearrange("p t b -> p (t b)").bitcast(I32))
         nc.sync.dma_start(value_list[:], voffs)
 
-        sink_col = keep.tile([P, 1], F32, name="sink_col")
-        nc.sync.dma_start(sink_col[:], sink[0])
         q_plane = keep.tile([P, PASSES, NQ], U8, name="q_plane", align_bytes=64)
-        nc.vector.memset(q_plane[:].bitcast(I32), 0)
-        q_rows = q_scales[0].bitcast(I32).rearrange("o f q -> f o q")
-        for j in range(4):
-            nc.sync.dma_start(q_plane[:].bitcast(I32)[32 * j : 32 * j + 4, :, :], q_rows[4 * j : 4 * j + 4, :, :])
+        nc.gpsimd.memset(q_plane[:].bitcast(I32), 0)
+        value_scale_pool = keep.tile([P, POOL_PAGES, DV], U8, name="value_scale_pool")
+        nc.gpsimd.memset(value_scale_pool[:].bitcast(I32), 0)
         ident = keep.tile([P, P], F32, name="ident")
         make_identity(nc, ident[:])
 
+        sink_col = keep.tile([P, 1], F32, name="sink_col")
+        nc.sync.dma_start(sink_col[:], sink[0])
+        q_codes = keep.tile([P, PASSES, NQ], I32, name="q_codes", align_bytes=64)
+        nc.sync.dma_start(q_codes[:], q_words[0].rearrange("o p q r -> p o (q r)").bitcast(I32))
+        q_rows = q_scales[0].bitcast(I32).rearrange("o f q -> f o q")
+        for j in range(4):
+            nc.sync.dma_start(q_plane[:].bitcast(I32)[32 * j : 32 * j + 4, :, :], q_rows[4 * j : 4 * j + 4, :, :])
+        value_pool = keep.tile([P, POOL_PAGES, DV], I32, name="value_pool")
+        nc.gpsimd.dma_start(value_pool[:], v_words.rearrange("u p e r -> p u (e r)").bitcast(I32))
+        v_rows = v_scales.bitcast(I32).rearrange("u f e -> f u e")
+        for j in range(4):
+            nc.gpsimd.dma_start(
+                value_scale_pool[:].bitcast(I32)[32 * j : 32 * j + 4, :, :], v_rows[4 * j : 4 * j + 4, :, :]
+            )
+
+        neg_sink = keep.tile([P, 1], F32, name="neg_sink")
         warm = keep.tile([P, 1], F32, name="warm")
         nc.scalar.activation(warm[:], sink_col[:], ACT.Exp, scale=0.0)
-
-        key_planes = [keep.tile([P, N], U8, name=f"key_plane{o}", align_bytes=64) for o in range(PASSES)]
-        for o in range(PASSES):
-            nc.vector.memset(key_planes[o][:].bitcast(I32), 0)
+        nc.scalar.activation(neg_sink[:], sink_col[:], ACT.Copy, scale=-1.0)
 
         key_scales_listed = keep.tile([P, N], U8, name="key_scales_listed")
         nc.vector.tensor_copy(key_scales_listed[:], key_scale_pool.indirect(key_list[:]))
+        key_planes = shared.tile([P, PASSES * N], U8, name="key_planes", align_bytes=64, offset=0)
         for o in range(PASSES):
             for j in range(4):
                 nc.sync.dma_start(
-                    key_planes[o][:].bitcast(I32)[32 * j : 32 * j + 4, :],
-                    key_scales_listed[:].bitcast(I32)[64 * o + 16 * j : 64 * o + 16 * (j + 1) : 4, :],
+                    key_planes[:].bitcast(I32)[32 * j : 32 * j + 4, o * N // 4 : (o + 1) * N // 4],
+                    key_scales_listed[:].bitcast(I32)[16 * o + 4 * j : 16 * o + 4 * (j + 1), :],
                 )
-
-        value_scale_pool = shared.tile([P, POOL_PAGES, DV], U8, name="value_scale_pool", offset=16384)
-        nc.vector.memset(value_scale_pool[:].bitcast(I32), 0)
-        v_rows = v_scales.bitcast(I32).rearrange("u f e -> f u e")
-        for j in range(4):
-            nc.sync.dma_start(value_scale_pool[:].bitcast(I32)[32 * j : 32 * j + 4, :, :], v_rows[4 * j : 4 * j + 4, :, :])
-        token_scale_pool = shared.tile([P, T], F32, name="token_scale_pool", offset=0)
+        token_scale_pool = shared.tile([P, T], F32, name="token_scale_pool", offset=T)
         nc.sync.dma_start(token_scale_pool[:], vs)
 
-        neg_maxima = shared.tile([P, PAGES + 1], F32, name="neg_maxima", offset=25600)
-        nc.vector.tensor_scalar(neg_maxima[:, PAGES:], sink_col[:], -1.0, None, ALU.mult)
+        def page_list(c):
+            return key_list[:, c * PAGE // 16 : (c + 1) * PAGE // 16]
 
-        neg_scores = []
-        for c in range(PAGES):
-            page_list = key_list[:, c * PAGE // 16 : (c + 1) * PAGE // 16]
-            key_pairs = shared.tile([P, PAGE], U32, name=f"key_pairs{c}", offset=17408 + 2048 * c)
-            page_pairs = key_pairs[:]
-            nc.vector.tensor_copy(page_pairs, key_pool[:].bitcast(U32).indirect(page_list))
-            key_codes = keep.tile([P, PASSES, PAGE], U16, name=f"key_codes{c}", align_bytes=64)
-            nc.vector.tensor_copy(key_codes[:], page_pairs.bitcast(U16).rearrange("p (n o) -> p o n", o=PASSES))
-            scores = psum.tile([P, PAGE], F32, name=f"scores{c}", tag=f"scores{c}")
+        key_pairs, scores, neg_scores, neg_maxima, token_scales = {}, {}, {}, {-1: neg_sink}, {}
+
+        def gather_keys(c):
+            key_pairs[c] = keep.tile([P, PAGE], U32, name=f"key_pairs{c}")
+            nc.vector.tensor_copy(key_pairs[c][:], key_pool[:].bitcast(U32).indirect(page_list(c)))
+
+        def score(c):
+            key_codes = shared.tile(
+                [P, PASSES, PAGE], U16, name=f"key_codes{c}", align_bytes=64, offset=20480 + 2048 * (c % 2)
+            )
+            nc.vector.tensor_copy(key_codes[:], key_pairs[c][:].bitcast(U16).rearrange("p (n o) -> p o n", o=PASSES))
+            scores[c] = psum.tile([P, PAGE], F32, name=f"scores{c}", tag=f"scores{c}")
             for o in range(PASSES):
                 nc.tensor.matmul_mx(
-                    out=scores[:],
+                    out=scores[c][:],
                     lhsT=q_codes[:, o, :].bitcast(FP8X4),
                     lhsT_scale=q_plane[:, o, :],
                     rhs=key_codes[:, o, :].bitcast(FP4X4),
-                    rhs_scale=key_planes[o][:, c * PAGE : (c + 1) * PAGE],
+                    rhs_scale=key_planes[:, o * N + c * PAGE : o * N + (c + 1) * PAGE],
                     start=(o == 0),
                     stop=(o == PASSES - 1),
                 )
-            negated = keep.tile([P, PAGE], F32, name=f"negated{c}")
-            nc.vector.tensor_scalar(
-                negated[:], scores[:], -1.0, None, ALU.mult, ALU.min, accum_out=neg_maxima[:, c : c + 1]
-            )
-            neg_scores.append(negated)
-        neg_max = keep.tile([P, 1], F32, name="neg_max")
-        nc.vector.tensor_reduce(neg_max[:], neg_maxima[:], AX.X, ALU.min)
 
-        value_codes = keep.tile([P, PAGES * DV], U32, name="value_codes", align_bytes=64)
+        def running_max(c):
+            neg_scores[c] = shared.tile([P, PAGE], F32, name=f"neg_scores{c}", offset=24576 + 2048 * c)
+            neg_maxima[c] = keep.tile([P, 1], F32, name=f"neg_max{c}")
+            nc.vector.tensor_scalar(
+                neg_scores[c][:], scores[c][:], -1.0, neg_maxima[c - 1][:], ALU.mult, ALU.min, accum_out=neg_maxima[c][:]
+            )
+
+        token_scale_offsets = [20480, 22528, 0, 2048]
+
+        def gather_token_scales(c):
+            token_scales[c] = shared.tile([P, PAGE], F32, name=f"token_scales{c}", offset=token_scale_offsets[c])
+            nc.vector.tensor_copy(token_scales[c][:], token_scale_pool[:].indirect(page_list(c)))
+
+        gather_keys(0)
+        gather_keys(1)
+        score(0)
+        gather_keys(2)
+        score(1)
+        gather_keys(3)
+        running_max(0)
+        score(2)
+        running_max(1)
+        score(3)
+        running_max(2)
+        gather_token_scales(0)
+        running_max(3)
+        neg_max = neg_maxima[PAGES - 1]
+        for c in range(1, PAGES):
+            gather_token_scales(c)
+
+        value_codes = shared.tile([P, PAGES * DV], U32, name="value_codes", align_bytes=64, offset=24576 + 2048)
         nc.vector.tensor_copy(
             value_codes[:], value_pool[:].rearrange("p u e -> p (u e)").bitcast(U32).indirect(value_list[:])
         )
-        value_scale_window = value_scale_pool[:].rearrange("p u e -> p (u e)")
-        early_plane = shared.tile([P, 2 * DV], U8, name="early_plane", align_bytes=64, offset=25600)
-        nc.vector.tensor_copy(early_plane[:], value_scale_window.indirect(value_list[:, 0:16]))
+        value_plane = shared.tile([P, PAGES * DV], U8, name="value_plane", align_bytes=64, offset=24576 + 4096)
+        nc.vector.tensor_copy(value_plane[:], value_scale_pool[:].rearrange("p u e -> p (u e)").indirect(value_list[:]))
 
-        exp_cuts = [0, 256, 512, 1024, 1536, 2048]
-        sums = keep.tile([P, len(exp_cuts)], F32, name="sums")
-        probs = {}
-        for i, (lo, hi) in enumerate(zip(exp_cuts, exp_cuts[1:])):
+        cuts = [0, 256, 512, 1024, 1536, 2048]
+        sums = keep.tile([P, len(cuts)], F32, name="sums")
+        weights = [keep.tile([P, PAGE], BF16, name=f"weights{c}") for c in range(PAGES)]
+        for i, (lo, hi) in enumerate(zip(cuts, cuts[1:])):
             c = lo // PAGE
-            probs[lo] = keep.tile([P, hi - lo], F32, name=f"probs{lo}")
+            cols = slice(lo - c * PAGE, hi - c * PAGE)
+            probs = keep.tile([P, hi - lo], F32, name=f"probs{lo}")
             nc.scalar.activation(
-                probs[lo][:],
-                neg_scores[c][:, lo - c * PAGE : hi - c * PAGE],
-                ACT.Exp,
-                bias=neg_max[:],
-                scale=-1.0,
-                accum_out=sums[:, i : i + 1],
+                probs[:], neg_scores[c][:, cols], ACT.Exp, bias=neg_max[:], scale=-1.0, accum_out=sums[:, i : i + 1]
             )
+            nc.gpsimd.tensor_tensor(weights[c][:, cols], probs[:], token_scales[c][:, cols], ALU.mult)
 
-        cuts = [0, 256, 512, 1024, 1536, 1920, 2048]
-        weights = {}
-        for lo, hi in zip(cuts, cuts[1:]):
-            start = max(e for e in exp_cuts if e <= lo)
-            weights[lo] = keep.tile([P, hi - lo], F32, name=f"weights{lo}")
-            nc.vector.tensor_tensor(
-                weights[lo][:],
-                token_scale_pool[:].indirect(key_list[:, lo // 16 : hi // 16]),
-                probs[start][:, lo - start : hi - start],
-                ALU.mult,
-            )
+        nc.scalar.activation(sums[:, len(cuts) - 1 :], sink_col[:], ACT.Exp, bias=neg_max[:])
+        total = keep.tile([P, 1], F32, name="total")
+        sums_again = keep.tile([P, len(cuts)], F32, name="sums_again")
+        nc.scalar.activation(sums_again[:], sums[:], ACT.Copy, accum_out=total[:])
 
         grouped = []
         for c in range(PAGES):
-            rounded = keep.tile([P, 2, P, 2], BF16, name=f"rounded{c}")
-            for lo, hi in zip(cuts, cuts[1:]):
-                if lo // PAGE == c:
-                    by_word = weights[lo][:].rearrange("q (s u e) -> q u s e", u=2, e=2)
-                    into = rounded[:, :, (lo - c * PAGE) // 4 : (hi - c * PAGE) // 4, :]
-                    if c < PAGES - 1:
-                        nc.scalar.copy(into, by_word)
-                    else:
-                        nc.vector.tensor_copy(into, by_word)
             turned = psum.tile([P, 2, NQ], F32, name=f"turned{c}")
+            words = weights[c][:].bitcast(F32)
             for u in range(2):
-                words = rounded[:, u, :, :].rearrange("q s e -> q (s e)").bitcast(F32)
-                nc.tensor.transpose(turned[:, u, :], words, ident[:])
+                nc.tensor.transpose(turned[:, u, :], words[:, u::2], ident[:])
             grouped.append(keep.tile([P, NQ, 4], BF16, name=f"grouped{c}", align_bytes=64))
             nc.scalar.copy(grouped[c][:].bitcast(F32), turned[:].rearrange("s u q -> s q u"))
 
-        nc.scalar.activation(sums[:, len(exp_cuts) - 1 :], sink_col[:], ACT.Exp, bias=neg_max[:])
-        total = keep.tile([P, 1], F32, name="total")
-        sums_again = keep.tile([P, len(exp_cuts)], F32, name="sums_again")
-        nc.scalar.activation(sums_again[:], sums[:], ACT.Copy, accum_out=total[:])
-
-        late_plane = shared.tile([P, 2 * DV], U8, name="late_plane", align_bytes=64, offset=64)
-        nc.vector.tensor_copy(late_plane[:], value_scale_window.indirect(value_list[:, 16:32]))
-        value_planes = [early_plane, late_plane]
-        inverse = shared.tile([P, 1], F32, name="inverse", offset=0)
+        inverse = keep.tile([P, 1], F32, name="inverse")
         nc.vector.reciprocal(inverse[:], total[:])
 
         acc = psum.tile([P, DV], F32, name="acc", tag="scores0")
@@ -198,7 +197,7 @@ def tile_attend_pkv4q_soft_sink_kernel(
                 lhsT=w_codes[:].bitcast(FP8X4),
                 lhsT_scale=w_plane[:],
                 rhs=value_codes[:, c * DV : (c + 1) * DV].bitcast(FP8X4),
-                rhs_scale=value_planes[c // 2][:, c % 2 * DV : (c % 2 + 1) * DV],
+                rhs_scale=value_plane[:, c * DV : (c + 1) * DV],
                 start=(c == 0),
                 stop=(c == PAGES - 1),
             )

@@ -39,8 +39,8 @@ def tile_attend_pkv4q_soft_sink_kernel(
         value_list = lists.tile([P, PAGES * DV // 16], U16, name="value_list")
         nc.sync.dma_start(key_list[:], offs)
 
-        key_scale_room = shared.tile([P, T + 64], U8, name="key_scale_room", align_bytes=64, offset=0)
-        key_scale_pool = key_scale_room[:, 0:T]
+        key_scale_room = shared.tile([P, T + 128], U8, name="key_scale_room", align_bytes=64, offset=T - 64)
+        key_scale_pool = key_scale_room[:, 64 : T + 64]
         nc.sync.dma_start(
             key_scale_pool.bitcast(I32)[0:32, :],
             k_scales.rearrange("o f t -> (o f) t").bitcast(I32),
@@ -66,11 +66,9 @@ def tile_attend_pkv4q_soft_sink_kernel(
         q_rows = q_scales[0].bitcast(I32).rearrange("o f q -> f o q")
         for j in range(4):
             nc.sync.dma_start(q_plane[:].bitcast(I32)[32 * j : 32 * j + 4, :, :], q_rows[4 * j : 4 * j + 4, :, :])
-        value_pool = keep.tile([P, POOL_PAGES, DV], I32, name="value_pool")
-        nc.gpsimd.dma_start(value_pool[:], v_words.rearrange("u p e r -> p u (e r)").bitcast(I32))
         v_rows = v_scales.bitcast(I32).rearrange("u f e -> f u e")
         for j in range(4):
-            nc.gpsimd.dma_start(
+            nc.sync.dma_start(
                 value_scale_pool[:].bitcast(I32)[32 * j : 32 * j + 4, :, :], v_rows[4 * j : 4 * j + 4, :, :]
             )
 
@@ -81,14 +79,16 @@ def tile_attend_pkv4q_soft_sink_kernel(
 
         key_scales_listed = keep.tile([P, N], U8, name="key_scales_listed")
         nc.vector.tensor_copy(key_scales_listed[:], key_scale_pool.indirect(key_list[:]))
-        key_planes = shared.tile([P, PASSES * N], U8, name="key_planes", align_bytes=64, offset=0)
+        key_planes = shared.tile([P, PASSES * N], U8, name="key_planes", align_bytes=64, offset=T)
         for o in range(PASSES):
             for j in range(4):
                 nc.sync.dma_start(
                     key_planes[:].bitcast(I32)[32 * j : 32 * j + 4, o * N // 4 : (o + 1) * N // 4],
                     key_scales_listed[:].bitcast(I32)[16 * o + 4 * j : 16 * o + 4 * (j + 1), :],
                 )
-        token_scale_pool = shared.tile([P, T], F32, name="token_scale_pool", offset=T)
+        value_pool = shared.tile([P, POOL_PAGES, DV], I32, name="value_pool", offset=0)
+        nc.sync.dma_start(value_pool[:], v_words.rearrange("u p e r -> p u (e r)").bitcast(I32))
+        token_scale_pool = shared.tile([P, T], F32, name="token_scale_pool", offset=2 * T)
         nc.sync.dma_start(token_scale_pool[:], vs)
 
         def page_list(c):
@@ -102,7 +102,7 @@ def tile_attend_pkv4q_soft_sink_kernel(
 
         def score(c):
             key_codes = shared.tile(
-                [P, PASSES, PAGE], U16, name=f"key_codes{c}", align_bytes=64, offset=20480 + 2048 * (c % 2)
+                [P, PASSES, PAGE], U16, name=f"key_codes{c}", align_bytes=64, offset=24576 + 2048 * (c % 2)
             )
             nc.vector.tensor_copy(key_codes[:], key_pairs[c][:].bitcast(U16).rearrange("p (n o) -> p o n", o=PASSES))
             scores[c] = psum.tile([P, PAGE], F32, name=f"scores{c}", tag=f"scores{c}")
@@ -118,13 +118,19 @@ def tile_attend_pkv4q_soft_sink_kernel(
                 )
 
         def running_max(c):
-            neg_scores[c] = shared.tile([P, PAGE], F32, name=f"neg_scores{c}", offset=24576 + 2048 * c)
+            neg_scores[c] = shared.tile([P, 4, P], F32, name=f"neg_scores{c}", offset=28672 + 2048 * c)
             neg_maxima[c] = keep.tile([P, 1], F32, name=f"neg_max{c}")
             nc.vector.tensor_scalar(
-                neg_scores[c][:], scores[c][:], -1.0, neg_maxima[c - 1][:], ALU.mult, ALU.min, accum_out=neg_maxima[c][:]
+                neg_scores[c][:],
+                scores[c][:].rearrange("q (s t) -> q t s", t=4),
+                -1.0,
+                neg_maxima[c - 1][:],
+                ALU.mult,
+                ALU.min,
+                accum_out=neg_maxima[c][:],
             )
 
-        token_scale_offsets = [20480, 22528, 0, 2048]
+        token_scale_offsets = [26624, T, T + 2048, 28672]
 
         def gather_token_scales(c):
             token_scales[c] = shared.tile([P, PAGE], F32, name=f"token_scales{c}", offset=token_scale_offsets[c])
@@ -141,66 +147,80 @@ def tile_attend_pkv4q_soft_sink_kernel(
         running_max(1)
         score(3)
         running_max(2)
-        gather_token_scales(0)
-        running_max(3)
-        neg_max = neg_maxima[PAGES - 1]
-        for c in range(1, PAGES):
-            gather_token_scales(c)
-
-        value_codes = shared.tile([P, PAGES * DV], U32, name="value_codes", align_bytes=64, offset=24576 + 2048)
+        value_codes = shared.tile([P, PAGES * DV], U32, name="value_codes", align_bytes=64, offset=24576)
         nc.vector.tensor_copy(
             value_codes[:], value_pool[:].rearrange("p u e -> p (u e)").bitcast(U32).indirect(value_list[:])
         )
-        value_plane = shared.tile([P, PAGES * DV], U8, name="value_plane", align_bytes=64, offset=24576 + 4096)
+        running_max(3)
+        neg_max = neg_maxima[PAGES - 1]
+
+        halves = [(0, 0, 2), (0, 2, 4), (1, 0, 4), (2, 0, 4), (3, 0, 4)]
+        sums = keep.tile([P, len(halves) + 1], F32, name="sums")
+        probs = [shared.tile([P, 4, P], F32, name=f"probs{c}", offset=36864 + 2048 * c) for c in range(PAGES)]
+        for i, (c, lo, hi) in enumerate(halves):
+            nc.scalar.activation(
+                probs[c][:, lo:hi, :],
+                neg_scores[c][:, lo:hi, :],
+                ACT.Exp,
+                bias=neg_max[:],
+                scale=-1.0,
+                accum_out=sums[:, i : i + 1],
+            )
+        turned = []
+        for c in range(PAGES):
+            turned.append(psum.tile([P, 4, NQ], F32, name=f"turned{c}", tag=f"scores{c}"))
+            for t in range(4):
+                nc.tensor.transpose(turned[c][:, t, :], probs[c][:, t, :], ident[:])
+
+        scale_cols = []
+        for c in range(PAGES):
+            gather_token_scales(c)
+            scales_turned = psum.tile([P, 4, P], F32, name=f"scales_turned{c}", tag=f"scales_turned{c % 3}")
+            for t in range(4):
+                nc.tensor.transpose(scales_turned[:, t, :], token_scales[c][:, t::4], ident[:])
+            scale_cols.append(shared.tile([P, 4], F32, name=f"scale_cols{c}", offset=28672 + 3 * 2048 + 32 * c))
+            nc.scalar.copy(scale_cols[c][:], scales_turned[:, :, 0])
+
+        value_plane = shared.tile([P, PAGES * DV], U8, name="value_plane", align_bytes=64, offset=26624)
         nc.vector.tensor_copy(value_plane[:], value_scale_pool[:].rearrange("p u e -> p (u e)").indirect(value_list[:]))
 
-        cuts = [0, 256, 512, 1024, 1536, 2048]
-        sums = keep.tile([P, len(cuts)], F32, name="sums")
-        weights = [keep.tile([P, PAGE], BF16, name=f"weights{c}") for c in range(PAGES)]
-        for i, (lo, hi) in enumerate(zip(cuts, cuts[1:])):
-            c = lo // PAGE
-            cols = slice(lo - c * PAGE, hi - c * PAGE)
-            probs = keep.tile([P, hi - lo], F32, name=f"probs{lo}")
-            nc.scalar.activation(
-                probs[:], neg_scores[c][:, cols], ACT.Exp, bias=neg_max[:], scale=-1.0, accum_out=sums[:, i : i + 1]
-            )
-            nc.gpsimd.tensor_tensor(weights[c][:, cols], probs[:], token_scales[c][:, cols], ALU.mult)
-
-        nc.scalar.activation(sums[:, len(cuts) - 1 :], sink_col[:], ACT.Exp, bias=neg_max[:])
+        nc.scalar.activation(sums[:, len(halves) :], sink_col[:], ACT.Exp, bias=neg_max[:])
         total = keep.tile([P, 1], F32, name="total")
-        sums_again = keep.tile([P, len(cuts)], F32, name="sums_again")
+        sums_again = keep.tile([P, len(halves) + 1], F32, name="sums_again")
         nc.scalar.activation(sums_again[:], sums[:], ACT.Copy, accum_out=total[:])
-
-        grouped = []
-        for c in range(PAGES):
-            turned = psum.tile([P, 2, NQ], F32, name=f"turned{c}")
-            words = weights[c][:].bitcast(F32)
-            for u in range(2):
-                nc.tensor.transpose(turned[:, u, :], words[:, u::2], ident[:])
-            grouped.append(keep.tile([P, NQ, 4], BF16, name=f"grouped{c}", align_bytes=64))
-            nc.scalar.copy(grouped[c][:].bitcast(F32), turned[:].rearrange("s u q -> s q u"))
-
-        inverse = keep.tile([P, 1], F32, name="inverse")
+        inverse = shared.tile([P, 1], F32, name="inverse", offset=28672 + 3 * 2048 + 32)
         nc.vector.reciprocal(inverse[:], total[:])
 
-        acc = psum.tile([P, DV], F32, name="acc", tag="scores0")
+        weights = keep.tile([P, PAGES, NQ, 4], BF16, name="weights", align_bytes=64)
         for c in range(PAGES):
-            w_codes = keep.tile([P, NQ], U32, name=f"w_codes{c}", align_bytes=64)
-            w_plane = keep.tile([P, NQ], U8, name=f"w_plane{c}", align_bytes=64)
+            nc.vector.tensor_tensor(
+                weights[:, c, :, :],
+                turned[c][:].rearrange("s t q -> s q t"),
+                scale_cols[c][:].unsqueeze(1).to_broadcast([P, NQ, 4]),
+                ALU.mult,
+            )
+
+        acc = psum.tile([P, DV], F32, name="acc")
+        for first, last, after in [(0, 2, 2), (2, 3, 3), (3, 4, 0)]:
+            width = (last - first) * NQ
+            w_codes = shared.tile([P, width], U32, name=f"w_codes{first}", align_bytes=64, offset=36864 + 2048 * after)
+            w_plane = keep.tile([P, width], U8, name=f"w_plane{first}", align_bytes=64)
             nc.vector.quantize_mx(
                 out=w_codes[:].bitcast(FP8X4),
                 scales=w_plane[:],
-                in_=grouped[c][:].rearrange("p q t -> p (q t)"),
+                in_=weights[:, first:last, :, :].rearrange("p c q t -> p (c q t)"),
             )
-            nc.tensor.matmul_mx(
-                out=acc[:],
-                lhsT=w_codes[:].bitcast(FP8X4),
-                lhsT_scale=w_plane[:],
-                rhs=value_codes[:, c * DV : (c + 1) * DV].bitcast(FP8X4),
-                rhs_scale=value_plane[:, c * DV : (c + 1) * DV],
-                start=(c == 0),
-                stop=(c == PAGES - 1),
-            )
+            for c in range(first, last):
+                cols = slice((c - first) * NQ, (c - first + 1) * NQ)
+                nc.tensor.matmul_mx(
+                    out=acc[:],
+                    lhsT=w_codes[:, cols].bitcast(FP8X4),
+                    lhsT_scale=w_plane[:, cols],
+                    rhs=value_codes[:, c * DV : (c + 1) * DV].bitcast(FP8X4),
+                    rhs_scale=value_plane[:, c * DV : (c + 1) * DV],
+                    start=(c == 0),
+                    stop=(c == PAGES - 1),
+                )
 
         result = keep.tile([P, DV], F32, name="result")
         nc.vector.tensor_scalar(result[:], acc[:], inverse[:], None, ALU.mult)

@@ -80,16 +80,16 @@ def tile_attend_pkv4q_soft_sink_kernel(
         key_scales_listed = keep.tile([P, N], U8, name="key_scales_listed")
         nc.vector.tensor_copy(key_scales_listed[:], key_scale_pool.indirect(key_list[:]))
         key_planes = shared.tile([P, PASSES * N], U8, name="key_planes", align_bytes=64, offset=T)
-        for o in range(PASSES):
+        for o in reversed(range(PASSES)):
             for j in range(4):
                 nc.sync.dma_start(
                     key_planes[:].bitcast(I32)[32 * j : 32 * j + 4, o * N // 4 : (o + 1) * N // 4],
                     key_scales_listed[:].bitcast(I32)[16 * o + 4 * j : 16 * o + 4 * (j + 1), :],
                 )
-        value_pool = shared.tile([P, POOL_PAGES, DV], I32, name="value_pool", offset=0)
-        nc.sync.dma_start(value_pool[:], v_words.rearrange("u p e r -> p u (e r)").bitcast(I32))
         token_scale_pool = shared.tile([P, T], F32, name="token_scale_pool", offset=2 * T)
         nc.sync.dma_start(token_scale_pool[:], vs)
+        value_pool = shared.tile([P, POOL_PAGES, DV], I32, name="value_pool", offset=0)
+        nc.sync.dma_start(value_pool[:], v_words.rearrange("u p e r -> p u (e r)").bitcast(I32))
 
         def page_list(c):
             return key_list[:, c * PAGE // 16 : (c + 1) * PAGE // 16]
@@ -102,9 +102,14 @@ def tile_attend_pkv4q_soft_sink_kernel(
 
         def score(c):
             key_codes = shared.tile(
-                [P, PASSES, PAGE], U16, name=f"key_codes{c}", align_bytes=64, offset=24576 + 2048 * (c % 2)
+                [P, PASSES, PAGE], U16, name=f"key_codes{c}", align_bytes=64, offset=24576 + 2048 * (c % 3)
             )
-            nc.vector.tensor_copy(key_codes[:], key_pairs[c][:].bitcast(U16).rearrange("p (n o) -> p o n", o=PASSES))
+            by_pass = key_pairs[c][:].bitcast(U16).rearrange("p (n o) -> p o n", o=PASSES)
+            if c < PAGES - 1:
+                nc.vector.tensor_copy(key_codes[:], by_pass)
+            else:
+                for o in range(PASSES):
+                    nc.vector.tensor_copy(key_codes[:, o, :], by_pass[:, o, :])
             scores[c] = psum.tile([P, PAGE], F32, name=f"scores{c}", tag=f"scores{c}")
             for o in range(PASSES):
                 nc.tensor.matmul_mx(
@@ -118,11 +123,11 @@ def tile_attend_pkv4q_soft_sink_kernel(
                 )
 
         def running_max(c):
-            neg_scores[c] = shared.tile([P, 4, P], F32, name=f"neg_scores{c}", offset=28672 + 2048 * c)
-            neg_maxima[c] = keep.tile([P, 1], F32, name=f"neg_max{c}")
+            neg_scores[c] = keep.tile([P, PAGE], F32, name=f"neg_scores{c}")
+            neg_maxima[c] = shared.tile([P, 1], F32, name=f"neg_max{c}", offset=40960 + 256 * c)
             nc.vector.tensor_scalar(
                 neg_scores[c][:],
-                scores[c][:].rearrange("q (s t) -> q t s", t=4),
+                scores[c][:],
                 -1.0,
                 neg_maxima[c - 1][:],
                 ALU.mult,
@@ -130,94 +135,113 @@ def tile_attend_pkv4q_soft_sink_kernel(
                 accum_out=neg_maxima[c][:],
             )
 
-        token_scale_offsets = [26624, T, T + 2048, 28672]
-
-        def gather_token_scales(c):
-            token_scales[c] = shared.tile([P, PAGE], F32, name=f"token_scales{c}", offset=token_scale_offsets[c])
-            nc.vector.tensor_copy(token_scales[c][:], token_scale_pool[:].indirect(page_list(c)))
-
         gather_keys(0)
         gather_keys(1)
         score(0)
         gather_keys(2)
         score(1)
         gather_keys(3)
-        running_max(0)
         score(2)
-        running_max(1)
+        running_max(0)
         score(3)
+        running_max(1)
         running_max(2)
-        value_codes = shared.tile([P, PAGES * DV], U32, name="value_codes", align_bytes=64, offset=24576)
-        nc.vector.tensor_copy(
-            value_codes[:], value_pool[:].rearrange("p u e -> p (u e)").bitcast(U32).indirect(value_list[:])
-        )
-        running_max(3)
+        value_scale_window = value_scale_pool[:].rearrange("p u e -> p (u e)")
+        value_planes = []
+        for h in range(2):
+            value_planes.append(
+                shared.tile([P, 2 * DV], U8, name=f"value_plane{h}", align_bytes=64, offset=[24576 + 4096, 40960 + 512][h])
+            )
+            nc.vector.tensor_copy(value_planes[h][:], value_scale_window.indirect(value_list[:, 16 * h : 16 * (h + 1)]))
+            if h == 0:
+                running_max(3)
         neg_max = neg_maxima[PAGES - 1]
 
-        halves = [(0, 0, 2), (0, 2, 4), (1, 0, 4), (2, 0, 4), (3, 0, 4)]
-        sums = keep.tile([P, len(halves) + 1], F32, name="sums")
-        probs = [shared.tile([P, 4, P], F32, name=f"probs{c}", offset=36864 + 2048 * c) for c in range(PAGES)]
-        for i, (c, lo, hi) in enumerate(halves):
+        exp_cuts = [0, 256, 512, 1024, 1536, 2048]
+        sums = shared.tile([P, len(exp_cuts)], F32, name="sums", offset=43008)
+        probs = {}
+        for i, (lo, hi) in enumerate(zip(exp_cuts, exp_cuts[1:])):
+            c = lo // PAGE
+            probs[lo] = keep.tile([P, hi - lo], F32, name=f"probs{lo}")
             nc.scalar.activation(
-                probs[c][:, lo:hi, :],
-                neg_scores[c][:, lo:hi, :],
+                probs[lo][:],
+                neg_scores[c][:, lo - c * PAGE : hi - c * PAGE],
                 ACT.Exp,
                 bias=neg_max[:],
                 scale=-1.0,
                 accum_out=sums[:, i : i + 1],
             )
-        turned = []
-        for c in range(PAGES):
-            turned.append(psum.tile([P, 4, NQ], F32, name=f"turned{c}", tag=f"scores{c}"))
-            for t in range(4):
-                nc.tensor.transpose(turned[c][:, t, :], probs[c][:, t, :], ident[:])
 
-        scale_cols = []
-        for c in range(PAGES):
-            gather_token_scales(c)
-            scales_turned = psum.tile([P, 4, P], F32, name=f"scales_turned{c}", tag=f"scales_turned{c % 3}")
-            for t in range(4):
-                nc.tensor.transpose(scales_turned[:, t, :], token_scales[c][:, t::4], ident[:])
-            scale_cols.append(shared.tile([P, 4], F32, name=f"scale_cols{c}", offset=28672 + 3 * 2048 + 32 * c))
-            nc.scalar.copy(scale_cols[c][:], scales_turned[:, :, 0])
-
-        value_plane = shared.tile([P, PAGES * DV], U8, name="value_plane", align_bytes=64, offset=26624)
-        nc.vector.tensor_copy(value_plane[:], value_scale_pool[:].rearrange("p u e -> p (u e)").indirect(value_list[:]))
-
-        nc.scalar.activation(sums[:, len(halves) :], sink_col[:], ACT.Exp, bias=neg_max[:])
+        nc.scalar.activation(sums[:, len(exp_cuts) - 1 :], sink_col[:], ACT.Exp, bias=neg_max[:])
         total = keep.tile([P, 1], F32, name="total")
-        sums_again = keep.tile([P, len(halves) + 1], F32, name="sums_again")
+        sums_again = keep.tile([P, len(exp_cuts)], F32, name="sums_again")
         nc.scalar.activation(sums_again[:], sums[:], ACT.Copy, accum_out=total[:])
-        inverse = shared.tile([P, 1], F32, name="inverse", offset=28672 + 3 * 2048 + 32)
-        nc.vector.reciprocal(inverse[:], total[:])
 
-        weights = keep.tile([P, PAGES, NQ, 4], BF16, name="weights", align_bytes=64)
-        for c in range(PAGES):
+        cuts = [0, 256, 512, 1024, 1536, 1920, 2048]
+        weights = [keep.tile([P, PAGE], F32, name=f"weights{c}") for c in range(PAGES)]
+        for lo, hi in zip(cuts, cuts[1:]):
+            c = lo // PAGE
+            start = max(e for e in exp_cuts if e <= lo)
             nc.vector.tensor_tensor(
-                weights[:, c, :, :],
-                turned[c][:].rearrange("s t q -> s q t"),
-                scale_cols[c][:].unsqueeze(1).to_broadcast([P, NQ, 4]),
+                weights[c][:, lo - c * PAGE : hi - c * PAGE],
+                token_scale_pool[:].indirect(key_list[:, lo // 16 : hi // 16]),
+                probs[start][:, lo - start : hi - start],
                 ALU.mult,
             )
 
+        grouped = keep.tile([P, PAGES, NQ, 4], BF16, name="grouped", align_bytes=64)
+        turned = []
+        for c in range(PAGES - 1):
+            turned.append(psum.tile([P, 4, NQ], F32, name=f"turned{c}", tag=f"scores{c}"))
+            for t in range(4):
+                nc.tensor.transpose(turned[c][:, t, :], weights[c][:, t::4], ident[:])
+
+        def round_turned(c):
+            nc.scalar.copy(grouped[:, c, :, :], turned[c][:].rearrange("s t q -> s q t"))
+
+        round_turned(0)
+        round_turned(1)
+        last = PAGES - 1
+        rounded = shared.tile([P, 2, P, 2], BF16, name="rounded", offset=45056)
+        for lo, hi in zip(cuts, cuts[1:]):
+            if lo // PAGE == last:
+                piece = weights[last][:, lo - last * PAGE : hi - last * PAGE]
+                nc.scalar.copy(
+                    rounded[:, :, (lo - last * PAGE) // 4 : (hi - last * PAGE) // 4, :],
+                    piece.rearrange("q (s u e) -> q u s e", u=2, e=2),
+                )
+        round_turned(2)
+        turned_words = psum.tile([P, 2, NQ], F32, name="turned_words", tag=f"scores{last}")
+        for u in range(2):
+            words = rounded[:, u, :, :].rearrange("q s e -> q (s e)").bitcast(F32)
+            nc.tensor.transpose(turned_words[:, u, :], words, ident[:])
+        nc.scalar.copy(grouped[:, last, :, :].bitcast(F32), turned_words[:].rearrange("s u q -> s q u"))
+
+        value_codes = shared.tile([P, PAGES * DV], U32, name="value_codes", align_bytes=64, offset=43008)
+        nc.vector.tensor_copy(
+            value_codes[:], value_pool[:].rearrange("p u e -> p (u e)").bitcast(U32).indirect(value_list[:])
+        )
+        inverse = keep.tile([P, 1], F32, name="inverse")
+        nc.vector.reciprocal(inverse[:], total[:])
+
         acc = psum.tile([P, DV], F32, name="acc")
-        for first, last, after in [(0, 2, 2), (2, 3, 3), (3, 4, 0)]:
-            width = (last - first) * NQ
-            w_codes = shared.tile([P, width], U32, name=f"w_codes{first}", align_bytes=64, offset=36864 + 2048 * after)
+        for first, end in [(0, 2), (2, 3), (3, 4)]:
+            width = (end - first) * NQ
+            w_codes = shared.tile([P, width], U32, name=f"w_codes{first}", align_bytes=64, offset=45056 + 512 * first)
             w_plane = keep.tile([P, width], U8, name=f"w_plane{first}", align_bytes=64)
             nc.vector.quantize_mx(
                 out=w_codes[:].bitcast(FP8X4),
                 scales=w_plane[:],
-                in_=weights[:, first:last, :, :].rearrange("p c q t -> p (c q t)"),
+                in_=grouped[:, first:end, :, :].rearrange("p c q t -> p (c q t)"),
             )
-            for c in range(first, last):
+            for c in range(first, end):
                 cols = slice((c - first) * NQ, (c - first + 1) * NQ)
                 nc.tensor.matmul_mx(
                     out=acc[:],
                     lhsT=w_codes[:, cols].bitcast(FP8X4),
                     lhsT_scale=w_plane[:, cols],
                     rhs=value_codes[:, c * DV : (c + 1) * DV].bitcast(FP8X4),
-                    rhs_scale=value_plane[:, c * DV : (c + 1) * DV],
+                    rhs_scale=value_planes[c // 2][:, c % 2 * DV : (c % 2 + 1) * DV],
                     start=(c == 0),
                     stop=(c == PAGES - 1),
                 )

@@ -60,19 +60,19 @@ def tile_attend_pkv4q_soft_sink_kernel(
         make_identity(nc, ident[:])
 
         sink_col = keep.tile([P, 1], F32, name="sink_col")
-        nc.sync.dma_start(sink_col[:], sink[0])
+        nc.scalar.dma_start(sink_col[:], sink[0])
         q_codes = keep.tile([P, PASSES, NQ], I32, name="q_codes", align_bytes=64)
         nc.sync.dma_start(q_codes[:], q_words[0].rearrange("o p q r -> p o (q r)").bitcast(I32))
         q_rows = q_scales[0].bitcast(I32).rearrange("o f q -> f o q")
         for j in range(4):
-            nc.sync.dma_start(q_plane[:].bitcast(I32)[32 * j : 32 * j + 4, :, :], q_rows[4 * j : 4 * j + 4, :, :])
+            nc.scalar.dma_start(q_plane[:].bitcast(I32)[32 * j : 32 * j + 4, :, :], q_rows[4 * j : 4 * j + 4, :, :])
         v_rows = v_scales.bitcast(I32).rearrange("u f e -> f u e")
         for j in range(4):
-            nc.sync.dma_start(
+            nc.scalar.dma_start(
                 value_scale_pool[:].bitcast(I32)[32 * j : 32 * j + 4, :, :], v_rows[4 * j : 4 * j + 4, :, :]
             )
 
-        neg_sink = keep.tile([P, 1], F32, name="neg_sink")
+        neg_sink = shared.tile([P, 1], F32, name="neg_sink", offset=40960)
         warm = keep.tile([P, 1], F32, name="warm")
         nc.scalar.activation(warm[:], sink_col[:], ACT.Exp, scale=0.0)
         nc.scalar.activation(neg_sink[:], sink_col[:], ACT.Copy, scale=-1.0)
@@ -124,16 +124,25 @@ def tile_attend_pkv4q_soft_sink_kernel(
 
         def running_max(c):
             neg_scores[c] = keep.tile([P, PAGE], F32, name=f"neg_scores{c}")
-            neg_maxima[c] = shared.tile([P, 1], F32, name=f"neg_max{c}", offset=40960 + 256 * c)
+            neg_maxima[c] = shared.tile([P, 64], F32, name=f"neg_max{c}", offset=40960 + 256 * (c + 1))
             nc.vector.tensor_scalar(
                 neg_scores[c][:],
                 scores[c][:],
                 -1.0,
-                neg_maxima[c - 1][:],
+                neg_maxima[c - 1][:, 0:1],
                 ALU.mult,
                 ALU.min,
-                accum_out=neg_maxima[c][:],
+                accum_out=neg_maxima[c][:, 0:1],
             )
+
+        value_scale_window = value_scale_pool[:].rearrange("p u e -> p (u e)")
+        value_planes = {}
+
+        def gather_value_scales(c):
+            value_planes[c] = shared.tile(
+                [P, DV], U8, name=f"value_plane{c}", align_bytes=64, offset=40960 + [0, 256, 768, 896][c]
+            )
+            nc.vector.tensor_copy(value_planes[c][:], value_scale_window.indirect(value_list[:, 8 * c : 8 * (c + 1)]))
 
         gather_keys(0)
         gather_keys(1)
@@ -145,19 +154,15 @@ def tile_attend_pkv4q_soft_sink_kernel(
         running_max(0)
         score(3)
         running_max(1)
+        gather_value_scales(0)
         running_max(2)
-        value_scale_window = value_scale_pool[:].rearrange("p u e -> p (u e)")
-        value_planes = []
-        for h in range(2):
-            value_planes.append(
-                shared.tile([P, 2 * DV], U8, name=f"value_plane{h}", align_bytes=64, offset=[24576 + 4096, 40960 + 512][h])
-            )
-            nc.vector.tensor_copy(value_planes[h][:], value_scale_window.indirect(value_list[:, 16 * h : 16 * (h + 1)]))
-            if h == 0:
-                running_max(3)
-        neg_max = neg_maxima[PAGES - 1]
+        gather_value_scales(1)
+        running_max(3)
+        gather_value_scales(2)
+        gather_value_scales(3)
+        neg_max = neg_maxima[PAGES - 1][:, 0:1]
 
-        exp_cuts = [0, 256, 512, 1024, 1536, 2048]
+        exp_cuts = [0, 128, 256, 512, 1024, 1536, 2048]
         sums = shared.tile([P, len(exp_cuts)], F32, name="sums", offset=43008)
         probs = {}
         for i, (lo, hi) in enumerate(zip(exp_cuts, exp_cuts[1:])):
@@ -167,17 +172,17 @@ def tile_attend_pkv4q_soft_sink_kernel(
                 probs[lo][:],
                 neg_scores[c][:, lo - c * PAGE : hi - c * PAGE],
                 ACT.Exp,
-                bias=neg_max[:],
+                bias=neg_max,
                 scale=-1.0,
                 accum_out=sums[:, i : i + 1],
             )
 
-        nc.scalar.activation(sums[:, len(exp_cuts) - 1 :], sink_col[:], ACT.Exp, bias=neg_max[:])
+        nc.scalar.activation(sums[:, len(exp_cuts) - 1 :], sink_col[:], ACT.Exp, bias=neg_max)
         total = keep.tile([P, 1], F32, name="total")
         sums_again = keep.tile([P, len(exp_cuts)], F32, name="sums_again")
         nc.scalar.activation(sums_again[:], sums[:], ACT.Copy, accum_out=total[:])
 
-        cuts = [0, 256, 512, 1024, 1536, 1920, 2048]
+        cuts = [0, 128, 256, 512, 1024, 1536, 1920, 2048]
         weights = [keep.tile([P, PAGE], F32, name=f"weights{c}") for c in range(PAGES)]
         for lo, hi in zip(cuts, cuts[1:]):
             c = lo // PAGE
@@ -241,7 +246,7 @@ def tile_attend_pkv4q_soft_sink_kernel(
                     lhsT=w_codes[:, cols].bitcast(FP8X4),
                     lhsT_scale=w_plane[:, cols],
                     rhs=value_codes[:, c * DV : (c + 1) * DV].bitcast(FP8X4),
-                    rhs_scale=value_planes[c // 2][:, c % 2 * DV : (c % 2 + 1) * DV],
+                    rhs_scale=value_planes[c][:],
                     start=(c == 0),
                     stop=(c == PAGES - 1),
                 )

@@ -45,17 +45,17 @@ def tile_attend_pkv4q_soft_sink_kernel(
             key_scale_pool.bitcast(I32)[0:32, :],
             k_scales.rearrange("o f t -> (o f) t").bitcast(I32),
         )
-        nc.vector.memset(key_scale_pool.bitcast(I32)[32:64, :], 0)
-        nc.vector.memset(key_scale_pool.bitcast(I32)[64:128, :], 0)
 
         key_pool = keep.tile([P, T], I32, name="key_pool", align_bytes=64)
         nc.sync.dma_start(key_pool[:], k_words[0].rearrange("p t b -> p (t b)").bitcast(I32))
         nc.sync.dma_start(value_list[:], voffs)
 
         q_plane = keep.tile([P, PASSES, NQ], U8, name="q_plane", align_bytes=64)
-        nc.gpsimd.memset(q_plane[:].bitcast(I32), 0)
+        nc.vector.memset(q_plane[:].bitcast(I32), 0)
         value_scale_pool = keep.tile([P, POOL_PAGES, DV], U8, name="value_scale_pool")
-        nc.gpsimd.memset(value_scale_pool[:].bitcast(I32), 0)
+        nc.vector.memset(value_scale_pool[:].bitcast(I32), 0)
+        nc.vector.memset(key_scale_pool.bitcast(I32)[32:64, :], 0)
+        nc.vector.memset(key_scale_pool.bitcast(I32)[64:128, :], 0)
         ident = keep.tile([P, P], F32, name="ident")
         make_identity(nc, ident[:])
 
@@ -72,10 +72,11 @@ def tile_attend_pkv4q_soft_sink_kernel(
                 value_scale_pool[:].bitcast(I32)[32 * j : 32 * j + 4, :, :], v_rows[4 * j : 4 * j + 4, :, :]
             )
 
-        neg_sink = shared.tile([P, 1], F32, name="neg_sink", offset=40960)
         warm = keep.tile([P, 1], F32, name="warm")
         nc.scalar.activation(warm[:], sink_col[:], ACT.Exp, scale=0.0)
-        nc.scalar.activation(neg_sink[:], sink_col[:], ACT.Copy, scale=-1.0)
+
+        maxima = shared.tile([P, PAGES + 1], F32, name="maxima", offset=40960)
+        nc.scalar.copy(maxima[:, PAGES:], sink_col[:])
 
         key_scales_listed = keep.tile([P, N], U8, name="key_scales_listed")
         nc.vector.tensor_copy(key_scales_listed[:], key_scale_pool.indirect(key_list[:]))
@@ -94,7 +95,7 @@ def tile_attend_pkv4q_soft_sink_kernel(
         def page_list(c):
             return key_list[:, c * PAGE // 16 : (c + 1) * PAGE // 16]
 
-        key_pairs, scores, neg_scores, neg_maxima, token_scales = {}, {}, {}, {-1: neg_sink}, {}
+        key_pairs, scores = {}, {}
 
         def gather_keys(c):
             key_pairs[c] = keep.tile([P, PAGE], U32, name=f"key_pairs{c}")
@@ -102,14 +103,10 @@ def tile_attend_pkv4q_soft_sink_kernel(
 
         def score(c):
             key_codes = shared.tile(
-                [P, PASSES, PAGE], U16, name=f"key_codes{c}", align_bytes=64, offset=24576 + 2048 * (c % 3)
+                [P, PASSES, PAGE], U16, name=f"key_codes{c}", align_bytes=64, offset=24576 + 2048 * c
             )
             by_pass = key_pairs[c][:].bitcast(U16).rearrange("p (n o) -> p o n", o=PASSES)
-            if c < PAGES - 1:
-                nc.vector.tensor_copy(key_codes[:], by_pass)
-            else:
-                for o in range(PASSES):
-                    nc.vector.tensor_copy(key_codes[:, o, :], by_pass[:, o, :])
+            nc.vector.tensor_copy(key_codes[:], by_pass)
             scores[c] = psum.tile([P, PAGE], F32, name=f"scores{c}", tag=f"scores{c}")
             for o in range(PASSES):
                 nc.tensor.matmul_mx(
@@ -122,67 +119,45 @@ def tile_attend_pkv4q_soft_sink_kernel(
                     stop=(o == PASSES - 1),
                 )
 
-        def running_max(c):
-            neg_scores[c] = keep.tile([P, PAGE], F32, name=f"neg_scores{c}")
-            neg_maxima[c] = shared.tile([P, 64], F32, name=f"neg_max{c}", offset=40960 + 256 * (c + 1))
-            nc.vector.tensor_scalar(
-                neg_scores[c][:],
-                scores[c][:],
-                -1.0,
-                neg_maxima[c - 1][:, 0:1],
-                ALU.mult,
-                ALU.min,
-                accum_out=neg_maxima[c][:, 0:1],
-            )
+        gather_keys(0)
+        for c in range(PAGES - 1):
+            gather_keys(c + 1)
+            score(c)
+        score(PAGES - 1)
+        for c in range(PAGES):
+            nc.vector.tensor_reduce(maxima[:, c : c + 1], scores[c][:], AX.X, ALU.max)
 
         value_scale_window = value_scale_pool[:].rearrange("p u e -> p (u e)")
-        value_planes = {}
+        first_plane = shared.tile([P, DV], U8, name="first_plane", align_bytes=64, offset=24576 + 2048 * 3)
+        later_planes = shared.tile([P, 2 * DV], U8, name="later_planes", align_bytes=64, offset=40960)
+        last_plane = shared.tile([P, DV], U8, name="last_plane", align_bytes=64, offset=44160)
+        value_planes = [first_plane[:], later_planes[:, :DV], later_planes[:, DV:], last_plane[:]]
+        neg_max = keep.tile([P, 1], F32, name="neg_max")
+        nc.vector.tensor_copy(first_plane[:], value_scale_window.indirect(value_list[:, : DV // 16]))
+        nc.vector.tensor_reduce(neg_max[:], maxima[:], AX.X, ALU.max, negate=True)
+        nc.vector.tensor_copy(later_planes[:], value_scale_window.indirect(value_list[:, DV // 16 : 3 * DV // 16]))
 
-        def gather_value_scales(c):
-            value_planes[c] = shared.tile(
-                [P, DV], U8, name=f"value_plane{c}", align_bytes=64, offset=40960 + [0, 256, 768, 896][c]
-            )
-            nc.vector.tensor_copy(value_planes[c][:], value_scale_window.indirect(value_list[:, 8 * c : 8 * (c + 1)]))
-
-        gather_keys(0)
-        gather_keys(1)
-        score(0)
-        gather_keys(2)
-        score(1)
-        gather_keys(3)
-        score(2)
-        running_max(0)
-        score(3)
-        running_max(1)
-        gather_value_scales(0)
-        running_max(2)
-        gather_value_scales(1)
-        running_max(3)
-        gather_value_scales(2)
-        gather_value_scales(3)
-        neg_max = neg_maxima[PAGES - 1][:, 0:1]
-
-        exp_cuts = [0, 128, 256, 512, 1024, 1536, 2048]
-        sums = shared.tile([P, len(exp_cuts)], F32, name="sums", offset=43008)
+        exp_cuts = [0, 256, 512, 1024, 1536, 2048]
+        sums_room = shared.tile([P, 64], F32, name="sums_room", offset=44032)
+        sums = sums_room[:, : len(exp_cuts)]
         probs = {}
         for i, (lo, hi) in enumerate(zip(exp_cuts, exp_cuts[1:])):
             c = lo // PAGE
             probs[lo] = keep.tile([P, hi - lo], F32, name=f"probs{lo}")
             nc.scalar.activation(
                 probs[lo][:],
-                neg_scores[c][:, lo - c * PAGE : hi - c * PAGE],
+                scores[c][:, lo - c * PAGE : hi - c * PAGE],
                 ACT.Exp,
-                bias=neg_max,
-                scale=-1.0,
+                bias=neg_max[:],
                 accum_out=sums[:, i : i + 1],
             )
 
-        nc.scalar.activation(sums[:, len(exp_cuts) - 1 :], sink_col[:], ACT.Exp, bias=neg_max)
+        nc.scalar.activation(sums[:, len(exp_cuts) - 1 :], sink_col[:], ACT.Exp, bias=neg_max[:])
         total = keep.tile([P, 1], F32, name="total")
         sums_again = keep.tile([P, len(exp_cuts)], F32, name="sums_again")
-        nc.scalar.activation(sums_again[:], sums[:], ACT.Copy, accum_out=total[:])
+        nc.scalar.activation(sums_again[:], sums, ACT.Copy, accum_out=total[:])
 
-        cuts = [0, 128, 256, 512, 1024, 1536, 1920, 2048]
+        cuts = [0, 256, 512, 1024, 1536, 1920, 2048]
         weights = [keep.tile([P, PAGE], F32, name=f"weights{c}") for c in range(PAGES)]
         for lo, hi in zip(cuts, cuts[1:]):
             c = lo // PAGE
@@ -197,7 +172,7 @@ def tile_attend_pkv4q_soft_sink_kernel(
         grouped = keep.tile([P, PAGES, NQ, 4], BF16, name="grouped", align_bytes=64)
         turned = []
         for c in range(PAGES - 1):
-            turned.append(psum.tile([P, 4, NQ], F32, name=f"turned{c}", tag=f"scores{c}"))
+            turned.append(psum.tile([P, 4, NQ], F32, name=f"turned{c}"))
             for t in range(4):
                 nc.tensor.transpose(turned[c][:, t, :], weights[c][:, t::4], ident[:])
 
@@ -216,16 +191,17 @@ def tile_attend_pkv4q_soft_sink_kernel(
                     piece.rearrange("q (s u e) -> q u s e", u=2, e=2),
                 )
         round_turned(2)
-        turned_words = psum.tile([P, 2, NQ], F32, name="turned_words", tag=f"scores{last}")
+        turned_words = psum.tile([P, 2, NQ], F32, name="turned_words", tag="scores0")
         for u in range(2):
             words = rounded[:, u, :, :].rearrange("q s e -> q (s e)").bitcast(F32)
             nc.tensor.transpose(turned_words[:, u, :], words, ident[:])
         nc.scalar.copy(grouped[:, last, :, :].bitcast(F32), turned_words[:].rearrange("s u q -> s q u"))
 
-        value_codes = shared.tile([P, PAGES * DV], U32, name="value_codes", align_bytes=64, offset=43008)
+        value_codes = shared.tile([P, PAGES * DV], U32, name="value_codes", align_bytes=64, offset=42048)
         nc.vector.tensor_copy(
             value_codes[:], value_pool[:].rearrange("p u e -> p (u e)").bitcast(U32).indirect(value_list[:])
         )
+        nc.vector.tensor_copy(last_plane[:], value_scale_window.indirect(value_list[:, 3 * DV // 16 :]))
         inverse = keep.tile([P, 1], F32, name="inverse")
         nc.vector.reciprocal(inverse[:], total[:])
 
@@ -246,7 +222,7 @@ def tile_attend_pkv4q_soft_sink_kernel(
                     lhsT=w_codes[:, cols].bitcast(FP8X4),
                     lhsT_scale=w_plane[:, cols],
                     rhs=value_codes[:, c * DV : (c + 1) * DV].bitcast(FP8X4),
-                    rhs_scale=value_planes[c][:],
+                    rhs_scale=value_planes[c],
                     start=(c == 0),
                     stop=(c == PAGES - 1),
                 )

@@ -72,8 +72,6 @@ def tile_attend_pkv4q_soft_sink_kernel(
                 value_scale_pool[:].bitcast(I32)[32 * j : 32 * j + 4, :, :], v_rows[4 * j : 4 * j + 4, :, :]
             )
 
-        warm = keep.tile([P, 1], F32, name="warm")
-        nc.scalar.activation(warm[:], sink_col[:], ACT.Exp, scale=0.0)
 
         maxima = shared.tile([P, PAGES + 1], F32, name="maxima", offset=40960)
         nc.scalar.copy(maxima[:, PAGES:], sink_col[:])
@@ -157,7 +155,7 @@ def tile_attend_pkv4q_soft_sink_kernel(
         sums_again = keep.tile([P, len(exp_cuts)], F32, name="sums_again")
         nc.scalar.activation(sums_again[:], sums, ACT.Copy, accum_out=total[:])
 
-        cuts = [0, 256, 512, 1024, 1536, 1920, 2048]
+        cuts = [0, 256, 512, 1024, 1536, 1856, 2048]
         weights = [keep.tile([P, PAGE], F32, name=f"weights{c}") for c in range(PAGES)]
         for lo, hi in zip(cuts, cuts[1:]):
             c = lo // PAGE
@@ -172,7 +170,7 @@ def tile_attend_pkv4q_soft_sink_kernel(
         grouped = keep.tile([P, PAGES, NQ, 4], BF16, name="grouped", align_bytes=64)
         turned = []
         for c in range(PAGES - 1):
-            turned.append(psum.tile([P, 4, NQ], F32, name=f"turned{c}"))
+            turned.append(psum.tile([P, 4, NQ], F32, name=f"turned{c}", tag=f"turned{c}"))
             for t in range(4):
                 nc.tensor.transpose(turned[c][:, t, :], weights[c][:, t::4], ident[:])
 
@@ -182,7 +180,7 @@ def tile_attend_pkv4q_soft_sink_kernel(
         round_turned(0)
         round_turned(1)
         last = PAGES - 1
-        rounded = shared.tile([P, 2, P, 2], BF16, name="rounded", offset=45056)
+        rounded = keep.tile([P, 2, P, 2], BF16, name="rounded")
         for lo, hi in zip(cuts, cuts[1:]):
             if lo // PAGE == last:
                 piece = weights[last][:, lo - last * PAGE : hi - last * PAGE]
@@ -205,10 +203,10 @@ def tile_attend_pkv4q_soft_sink_kernel(
         inverse = keep.tile([P, 1], F32, name="inverse")
         nc.vector.reciprocal(inverse[:], total[:])
 
-        acc = psum.tile([P, DV], F32, name="acc")
+        acc = psum.tile([P, DV], F32, name="acc", tag="turned2")
         for first, end in [(0, 2), (2, 3), (3, 4)]:
             width = (end - first) * NQ
-            w_codes = shared.tile([P, width], U32, name=f"w_codes{first}", align_bytes=64, offset=45056 + 512 * first)
+            w_codes = keep.tile([P, width], U32, name=f"w_codes{first}", align_bytes=64)
             w_plane = keep.tile([P, width], U8, name=f"w_plane{first}", align_bytes=64)
             nc.vector.quantize_mx(
                 out=w_codes[:].bitcast(FP8X4),

@@ -39,65 +39,79 @@ def tile_attend_pkv4q_soft_sink_kernel(
         value_list = lists.tile([P, PAGES * DV // 16], U16, name="value_list")
         nc.sync.dma_start(key_list[:], offs)
 
-        key_scale_room = shared.tile([P, T + 128], U8, name="key_scale_room", align_bytes=64, offset=T - 64)
+        key_scale_room = shared.tile([P, T + 192], U8, name="key_scale_room", align_bytes=64, offset=T - 64)
         key_scale_pool = key_scale_room[:, 64 : T + 64]
         nc.sync.dma_start(
             key_scale_pool.bitcast(I32)[0:32, :],
             k_scales.rearrange("o f t -> (o f) t").bitcast(I32),
         )
+        token_scale_pool = keep.tile([P, T], F32, name="token_scale_pool")
+        nc.scalar.dma_start(token_scale_pool[P - 1 :, :], vs[0:1, :])
 
         key_pool = keep.tile([P, T], I32, name="key_pool", align_bytes=64)
         nc.sync.dma_start(key_pool[:], k_words[0].rearrange("p t b -> p (t b)").bitcast(I32))
-        nc.sync.dma_start(value_list[:], voffs)
 
         q_plane = keep.tile([P, PASSES, NQ], U8, name="q_plane", align_bytes=64)
-        nc.vector.memset(q_plane[:].bitcast(I32), 0)
-        value_scale_pool = keep.tile([P, POOL_PAGES, DV], U8, name="value_scale_pool")
-        nc.vector.memset(value_scale_pool[:].bitcast(I32), 0)
+        nc.gpsimd.memset(q_plane[:].bitcast(I32), 0)
         nc.vector.memset(key_scale_pool.bitcast(I32)[32:64, :], 0)
         nc.vector.memset(key_scale_pool.bitcast(I32)[64:128, :], 0)
+        nc.vector.memset(token_scale_pool[:].bitcast(I32)[: P - 1, :], 0)
         ident = keep.tile([P, P], F32, name="ident")
         make_identity(nc, ident[:])
 
-        sink_col = keep.tile([P, 1], F32, name="sink_col")
-        nc.scalar.dma_start(sink_col[:], sink[0])
         q_codes = keep.tile([P, PASSES, NQ], I32, name="q_codes", align_bytes=64)
         nc.sync.dma_start(q_codes[:], q_words[0].rearrange("o p q r -> p o (q r)").bitcast(I32))
+        nc.sync.dma_start(value_list[:], voffs)
         q_rows = q_scales[0].bitcast(I32).rearrange("o f q -> f o q")
         for j in range(4):
             nc.scalar.dma_start(q_plane[:].bitcast(I32)[32 * j : 32 * j + 4, :, :], q_rows[4 * j : 4 * j + 4, :, :])
-        v_rows = v_scales.bitcast(I32).rearrange("u f e -> f u e")
-        for j in range(4):
-            nc.scalar.dma_start(
-                value_scale_pool[:].bitcast(I32)[32 * j : 32 * j + 4, :, :], v_rows[4 * j : 4 * j + 4, :, :]
-            )
-
-
-        maxima = shared.tile([P, PAGES + 1], F32, name="maxima", offset=40960)
-        nc.scalar.copy(maxima[:, PAGES:], sink_col[:])
 
         key_scales_listed = keep.tile([P, N], U8, name="key_scales_listed")
         nc.vector.tensor_copy(key_scales_listed[:], key_scale_pool.indirect(key_list[:]))
         key_planes = shared.tile([P, PASSES * N], U8, name="key_planes", align_bytes=64, offset=T)
         for o in reversed(range(PASSES)):
-            for j in range(4):
+            for j in (0, 2, 1, 3):
                 nc.sync.dma_start(
                     key_planes[:].bitcast(I32)[32 * j : 32 * j + 4, o * N // 4 : (o + 1) * N // 4],
                     key_scales_listed[:].bitcast(I32)[16 * o + 4 * j : 16 * o + 4 * (j + 1), :],
                 )
-        token_scale_pool = shared.tile([P, T], F32, name="token_scale_pool", offset=2 * T)
-        nc.sync.dma_start(token_scale_pool[:], vs)
+        sink_col = shared.tile([P, 1], F32, name="sink_col", offset=2 * T)
+        nc.sync.dma_start(sink_col[:], sink[0])
+        value_scale_pool = shared.tile([P, POOL_PAGES, DV], U8, name="value_scale_pool", offset=2 * T + 64)
+        nc.gpsimd.memset(value_scale_pool[:].bitcast(I32), 0)
+        v_rows = v_scales.bitcast(I32).rearrange("u f e -> f u e")
+        for j in range(4):
+            nc.sync.dma_start(
+                value_scale_pool[:].bitcast(I32)[32 * j : 32 * j + 4, :, :], v_rows[4 * j : 4 * j + 4, :, :]
+            )
         value_pool = shared.tile([P, POOL_PAGES, DV], I32, name="value_pool", offset=0)
         nc.sync.dma_start(value_pool[:], v_words.rearrange("u p e r -> p u (e r)").bitcast(I32))
 
-        def page_list(c):
-            return key_list[:, c * PAGE // 16 : (c + 1) * PAGE // 16]
+        def list_of(first, end):
+            return key_list[:, first * PAGE // 16 : end * PAGE // 16]
+
+        token_columns = {}
+
+        def gather_token_scales(listed, first, end):
+            nc.vector.tensor_copy(listed[:], token_scale_pool[:].indirect(list_of(first, end)))
+            for c in range(first, end):
+                token_columns[c] = keep.tile([P, 4], F32, name=f"token_columns{c}")
+                row = listed[P - 1 :, (c - first) * PAGE : (c - first + 1) * PAGE]
+                nc.sync.dma_start(token_columns[c][:], row.rearrange("o (s t) -> o s t", t=4))
+
+        last = PAGES - 1
+        early_scales = keep.tile([P, last * PAGE], F32, name="early_scales")
+        gather_token_scales(early_scales, 0, last)
+
+        maxima_room = shared.tile([P, 256], F32, name="maxima_room", offset=40960)
+        maxima = maxima_room[:, : PAGES + 1]
+        nc.scalar.copy(maxima[:, PAGES:], sink_col[:])
 
         key_pairs, scores = {}, {}
 
         def gather_keys(c):
             key_pairs[c] = keep.tile([P, PAGE], U32, name=f"key_pairs{c}")
-            nc.vector.tensor_copy(key_pairs[c][:], key_pool[:].bitcast(U32).indirect(page_list(c)))
+            nc.vector.tensor_copy(key_pairs[c][:], key_pool[:].bitcast(U32).indirect(list_of(c, c + 1)))
 
         def score(c):
             key_codes = shared.tile(
@@ -118,112 +132,87 @@ def tile_attend_pkv4q_soft_sink_kernel(
                 )
 
         gather_keys(0)
-        for c in range(PAGES - 1):
+        for c in range(last):
             gather_keys(c + 1)
             score(c)
-        score(PAGES - 1)
+        score(last)
         for c in range(PAGES):
             nc.vector.tensor_reduce(maxima[:, c : c + 1], scores[c][:], AX.X, ALU.max)
 
         value_scale_window = value_scale_pool[:].rearrange("p u e -> p (u e)")
-        first_plane = shared.tile([P, DV], U8, name="first_plane", align_bytes=64, offset=24576 + 2048 * 3)
-        later_planes = shared.tile([P, 2 * DV], U8, name="later_planes", align_bytes=64, offset=40960)
-        last_plane = shared.tile([P, DV], U8, name="last_plane", align_bytes=64, offset=44160)
-        value_planes = [first_plane[:], later_planes[:, :DV], later_planes[:, DV:], last_plane[:]]
+        first_plane = shared.tile([P, DV], U8, name="first_plane", align_bytes=64, offset=24576 + 2048 * last)
+        later_planes = shared.tile([P, last * DV], U8, name="later_planes", align_bytes=64, offset=41088)
+        value_planes = [first_plane[:]] + [later_planes[:, c * DV : (c + 1) * DV] for c in range(last)]
         neg_max = keep.tile([P, 1], F32, name="neg_max")
         nc.vector.tensor_copy(first_plane[:], value_scale_window.indirect(value_list[:, : DV // 16]))
-        nc.vector.tensor_reduce(neg_max[:], maxima[:], AX.X, ALU.max, negate=True)
-        nc.vector.tensor_copy(later_planes[:], value_scale_window.indirect(value_list[:, DV // 16 : 3 * DV // 16]))
-
-        exp_cuts = [0, 256, 512, 1024, 1536, 2048]
-        sums_room = shared.tile([P, 64], F32, name="sums_room", offset=44032)
-        sums = sums_room[:, : len(exp_cuts)]
-        probs = {}
-        for i, (lo, hi) in enumerate(zip(exp_cuts, exp_cuts[1:])):
-            c = lo // PAGE
-            probs[lo] = keep.tile([P, hi - lo], F32, name=f"probs{lo}")
-            nc.scalar.activation(
-                probs[lo][:],
-                scores[c][:, lo - c * PAGE : hi - c * PAGE],
-                ACT.Exp,
-                bias=neg_max[:],
-                accum_out=sums[:, i : i + 1],
-            )
-
-        nc.scalar.activation(sums[:, len(exp_cuts) - 1 :], sink_col[:], ACT.Exp, bias=neg_max[:])
-        total = keep.tile([P, 1], F32, name="total")
-        sums_again = keep.tile([P, len(exp_cuts)], F32, name="sums_again")
-        nc.scalar.activation(sums_again[:], sums, ACT.Copy, accum_out=total[:])
-
-        cuts = [0, 256, 512, 1024, 1536, 1856, 2048]
-        weights = [keep.tile([P, PAGE], F32, name=f"weights{c}") for c in range(PAGES)]
-        for lo, hi in zip(cuts, cuts[1:]):
-            c = lo // PAGE
-            start = max(e for e in exp_cuts if e <= lo)
-            nc.vector.tensor_tensor(
-                weights[c][:, lo - c * PAGE : hi - c * PAGE],
-                token_scale_pool[:].indirect(key_list[:, lo // 16 : hi // 16]),
-                probs[start][:, lo - start : hi - start],
-                ALU.mult,
-            )
-
-        grouped = keep.tile([P, PAGES, NQ, 4], BF16, name="grouped", align_bytes=64)
-        turned = []
-        for c in range(PAGES - 1):
-            turned.append(psum.tile([P, 4, NQ], F32, name=f"turned{c}", tag=f"turned{c}"))
-            for t in range(4):
-                nc.tensor.transpose(turned[c][:, t, :], weights[c][:, t::4], ident[:])
-
-        def round_turned(c):
-            nc.scalar.copy(grouped[:, c, :, :], turned[c][:].rearrange("s t q -> s q t"))
-
-        round_turned(0)
-        round_turned(1)
-        last = PAGES - 1
-        rounded = keep.tile([P, 2, P, 2], BF16, name="rounded")
-        for lo, hi in zip(cuts, cuts[1:]):
-            if lo // PAGE == last:
-                piece = weights[last][:, lo - last * PAGE : hi - last * PAGE]
-                nc.scalar.copy(
-                    rounded[:, :, (lo - last * PAGE) // 4 : (hi - last * PAGE) // 4, :],
-                    piece.rearrange("q (s u e) -> q u s e", u=2, e=2),
-                )
-        round_turned(2)
-        turned_words = psum.tile([P, 2, NQ], F32, name="turned_words", tag="scores0")
-        for u in range(2):
-            words = rounded[:, u, :, :].rearrange("q s e -> q (s e)").bitcast(F32)
-            nc.tensor.transpose(turned_words[:, u, :], words, ident[:])
-        nc.scalar.copy(grouped[:, last, :, :].bitcast(F32), turned_words[:].rearrange("s u q -> s q u"))
-
-        value_codes = shared.tile([P, PAGES * DV], U32, name="value_codes", align_bytes=64, offset=42048)
+        nc.vector.tensor_reduce(neg_max[:], maxima, AX.X, ALU.max, negate=True)
+        late_scales = shared.tile([P, PAGE], F32, name="late_scales", offset=38976)
+        gather_token_scales(late_scales, last, PAGES)
+        value_codes = shared.tile([P, PAGES * DV], U32, name="value_codes", align_bytes=64, offset=41536)
         nc.vector.tensor_copy(
             value_codes[:], value_pool[:].rearrange("p u e -> p (u e)").bitcast(U32).indirect(value_list[:])
         )
-        nc.vector.tensor_copy(last_plane[:], value_scale_window.indirect(value_list[:, 3 * DV // 16 :]))
-        inverse = keep.tile([P, 1], F32, name="inverse")
+        nc.vector.tensor_copy(later_planes[:], value_scale_window.indirect(value_list[:, DV // 16 :]))
+
+        sums = keep.tile([P, PAGES + 1], F32, name="sums")
+        turned = []
+        for c in range(PAGES):
+            probs = shared.tile([P, 4, P], F32, name=f"probs{c}", align_bytes=64, offset=49152 + 2048 * c)
+            nc.scalar.activation(
+                probs[:].rearrange("q t s -> q s t"),
+                scores[c][:].rearrange("q (s t) -> q s t", t=4),
+                ACT.Exp,
+                bias=neg_max[:],
+                accum_out=sums[:, c : c + 1],
+            )
+            turned.append(psum.tile([P, 4, NQ], F32, name=f"turned{c}", tag=f"turned{c}"))
+            for t in range(4):
+                nc.tensor.transpose(turned[c][:, t, :], probs[:, t, :], ident[:])
+        nc.scalar.activation(sums[:, PAGES:], sink_col[:], ACT.Exp, bias=neg_max[:])
+        total = keep.tile([P, 1], F32, name="total")
+        sums_again = keep.tile([P, PAGES + 1], F32, name="sums_again")
+        nc.scalar.activation(sums_again[:], sums[:], ACT.Copy, accum_out=total[:])
+
+        grouped, w_codes, w_plane = {}, {}, {}
+
+        def weigh(c):
+            grouped[c] = keep.tile([P, NQ, 4], BF16, name=f"grouped{c}", align_bytes=64)
+            nc.vector.tensor_tensor(
+                grouped[c][:],
+                turned[c][:].rearrange("s t q -> s q t"),
+                token_columns[c][:].unsqueeze(1).to_broadcast([P, NQ, 4]),
+                ALU.mult,
+            )
+
+        def quantise(c):
+            behind = 49152 + 2048 * (c + 1)
+            w_codes[c] = shared.tile([P, NQ], U32, name=f"w_codes{c}", align_bytes=64, offset=behind)
+            w_plane[c] = shared.tile([P, NQ], U8, name=f"w_plane{c}", align_bytes=64, offset=behind + 512)
+            nc.vector.quantize_mx(
+                out=w_codes[c][:].bitcast(FP8X4),
+                scales=w_plane[c][:],
+                in_=grouped[c][:].rearrange("p q t -> p (q t)"),
+            )
+
+        weigh(0)
+        for c in range(last):
+            weigh(c + 1)
+            quantise(c)
+        inverse = shared.tile([P, 1], F32, name="inverse", offset=49152 + 2048 * last + 1024)
         nc.vector.reciprocal(inverse[:], total[:])
+        quantise(last)
 
         acc = psum.tile([P, DV], F32, name="acc", tag="turned2")
-        for first, end in [(0, 2), (2, 3), (3, 4)]:
-            width = (end - first) * NQ
-            w_codes = keep.tile([P, width], U32, name=f"w_codes{first}", align_bytes=64)
-            w_plane = keep.tile([P, width], U8, name=f"w_plane{first}", align_bytes=64)
-            nc.vector.quantize_mx(
-                out=w_codes[:].bitcast(FP8X4),
-                scales=w_plane[:],
-                in_=grouped[:, first:end, :, :].rearrange("p c q t -> p (c q t)"),
+        for c in range(PAGES):
+            nc.tensor.matmul_mx(
+                out=acc[:],
+                lhsT=w_codes[c][:].bitcast(FP8X4),
+                lhsT_scale=w_plane[c][:],
+                rhs=value_codes[:, c * DV : (c + 1) * DV].bitcast(FP8X4),
+                rhs_scale=value_planes[c],
+                start=(c == 0),
+                stop=(c == last),
             )
-            for c in range(first, end):
-                cols = slice((c - first) * NQ, (c - first + 1) * NQ)
-                nc.tensor.matmul_mx(
-                    out=acc[:],
-                    lhsT=w_codes[:, cols].bitcast(FP8X4),
-                    lhsT_scale=w_plane[:, cols],
-                    rhs=value_codes[:, c * DV : (c + 1) * DV].bitcast(FP8X4),
-                    rhs_scale=value_planes[c],
-                    start=(c == 0),
-                    stop=(c == PAGES - 1),
-                )
 
         result = keep.tile([P, DV], F32, name="result")
         nc.vector.tensor_scalar(result[:], acc[:], inverse[:], None, ALU.mult)

@@ -53,11 +53,12 @@ def tile_attend_pkv4q_soft_sink_kernel(
 
         q_plane = keep.tile([P, PASSES, NQ], U8, name="q_plane", align_bytes=64)
         nc.gpsimd.memset(q_plane[:].bitcast(I32), 0)
-        nc.vector.memset(key_scale_pool.bitcast(I32)[32:64, :], 0)
-        nc.vector.memset(key_scale_pool.bitcast(I32)[64:128, :], 0)
-        nc.vector.memset(token_scale_pool[:].bitcast(I32)[: P - 1, :], 0)
         ident = keep.tile([P, P], F32, name="ident")
         make_identity(nc, ident[:])
+        nc.gpsimd.memset(token_scale_pool[:].bitcast(I32)[: P - 1, :], 0)
+        odd_run = key_scale_room[:, 60 : T + 64].bitcast(I32)
+        nc.vector.memset(odd_run[32:64, :], 0)
+        nc.vector.memset(odd_run[64:128, :], 0)
 
         q_codes = keep.tile([P, PASSES, NQ], I32, name="q_codes", align_bytes=64)
         nc.sync.dma_start(q_codes[:], q_words[0].rearrange("o p q r -> p o (q r)").bitcast(I32))
@@ -100,8 +101,8 @@ def tile_attend_pkv4q_soft_sink_kernel(
                 nc.sync.dma_start(token_columns[c][:], row.rearrange("o (s t) -> o s t", t=4))
 
         last = PAGES - 1
-        early_scales = keep.tile([P, last * PAGE], F32, name="early_scales")
-        gather_token_scales(early_scales, 0, last)
+        token_scales_listed = keep.tile([P, N], F32, name="token_scales_listed")
+        gather_token_scales(token_scales_listed, 0, PAGES)
 
         maxima_room = shared.tile([P, 256], F32, name="maxima_room", offset=40960)
         maxima = maxima_room[:, : PAGES + 1]
@@ -146,8 +147,6 @@ def tile_attend_pkv4q_soft_sink_kernel(
         neg_max = keep.tile([P, 1], F32, name="neg_max")
         nc.vector.tensor_copy(first_plane[:], value_scale_window.indirect(value_list[:, : DV // 16]))
         nc.vector.tensor_reduce(neg_max[:], maxima, AX.X, ALU.max, negate=True)
-        late_scales = shared.tile([P, PAGE], F32, name="late_scales", offset=38976)
-        gather_token_scales(late_scales, last, PAGES)
         value_codes = shared.tile([P, PAGES * DV], U32, name="value_codes", align_bytes=64, offset=41536)
         nc.vector.tensor_copy(
             value_codes[:], value_pool[:].rearrange("p u e -> p (u e)").bitcast(U32).indirect(value_list[:])

@@ -37,35 +37,31 @@ def tile_attend_pkv4q_soft_sink_kernel(
 
         key_list = lists.tile([P, N // 16], U16, name="key_list")
         value_list = lists.tile([P, PAGES * DV // 16], U16, name="value_list")
-        nc.sync.dma_start(key_list[:], offs)
-
         key_scale_room = shared.tile([P, T + 192], U8, name="key_scale_room", align_bytes=64, offset=T - 64)
         key_scale_pool = key_scale_room[:, 64 : T + 64]
         nc.sync.dma_start(
             key_scale_pool.bitcast(I32)[0:32, :],
             k_scales.rearrange("o f t -> (o f) t").bitcast(I32),
         )
+        nc.sync.dma_start(key_list[:], offs)
         token_scale_pool = keep.tile([P, T], F32, name="token_scale_pool")
         nc.scalar.dma_start(token_scale_pool[P - 1 :, :], vs[0:1, :])
 
-        key_pool = keep.tile([P, T], I32, name="key_pool", align_bytes=64)
-        nc.sync.dma_start(key_pool[:], k_words[0].rearrange("p t b -> p (t b)").bitcast(I32))
-
         q_plane = keep.tile([P, PASSES, NQ], U8, name="q_plane", align_bytes=64)
         nc.gpsimd.memset(q_plane[:].bitcast(I32), 0)
-        ident = keep.tile([P, P], F32, name="ident")
-        make_identity(nc, ident[:])
         nc.gpsimd.memset(token_scale_pool[:].bitcast(I32)[: P - 1, :], 0)
         odd_run = key_scale_room[:, 60 : T + 64].bitcast(I32)
         nc.vector.memset(odd_run[32:64, :], 0)
         nc.vector.memset(odd_run[64:128, :], 0)
 
+        q_rows = q_scales[0].bitcast(I32).rearrange("o f q -> f o q")
+        for j in range(4):
+            nc.sync.dma_start(q_plane[:].bitcast(I32)[32 * j : 32 * j + 4, :, :], q_rows[4 * j : 4 * j + 4, :, :])
+        key_pool = keep.tile([P, T], I32, name="key_pool", align_bytes=64)
+        nc.sync.dma_start(key_pool[:], k_words[0].rearrange("p t b -> p (t b)").bitcast(I32))
         q_codes = keep.tile([P, PASSES, NQ], I32, name="q_codes", align_bytes=64)
         nc.sync.dma_start(q_codes[:], q_words[0].rearrange("o p q r -> p o (q r)").bitcast(I32))
         nc.sync.dma_start(value_list[:], voffs)
-        q_rows = q_scales[0].bitcast(I32).rearrange("o f q -> f o q")
-        for j in range(4):
-            nc.scalar.dma_start(q_plane[:].bitcast(I32)[32 * j : 32 * j + 4, :, :], q_rows[4 * j : 4 * j + 4, :, :])
 
         key_scales_listed = keep.tile([P, N], U8, name="key_scales_listed")
         nc.vector.tensor_copy(key_scales_listed[:], key_scale_pool.indirect(key_list[:]))
@@ -153,23 +149,27 @@ def tile_attend_pkv4q_soft_sink_kernel(
         )
         nc.vector.tensor_copy(later_planes[:], value_scale_window.indirect(value_list[:, DV // 16 :]))
 
-        sums = keep.tile([P, PAGES + 1], F32, name="sums")
-        turned = []
-        for c in range(PAGES):
-            probs = shared.tile([P, 4, P], F32, name=f"probs{c}", align_bytes=64, offset=49152 + 2048 * c)
+        ident = shared.tile([P, P], F32, name="ident", offset=24576 + 2048 * (last - 1))
+        make_identity(nc, ident[:])
+        pieces = [(c, 0, 4) for c in range(last)] + [(last, 0, 2), (last, 2, 4)]
+        sums = keep.tile([P, len(pieces) + 1], F32, name="sums")
+        turned = [psum.tile([P, 4, NQ], F32, name=f"turned{c}", tag=f"turned{c}") for c in range(PAGES)]
+        for i, (c, first, end) in enumerate(pieces):
+            probs = shared.tile(
+                [P, end - first, P], F32, name=f"probs{i}", align_bytes=64, offset=49152 + 2048 * c + 512 * first
+            )
             nc.scalar.activation(
                 probs[:].rearrange("q t s -> q s t"),
-                scores[c][:].rearrange("q (s t) -> q s t", t=4),
+                scores[c][:].rearrange("q (s t) -> q s t", t=4)[:, :, first:end],
                 ACT.Exp,
                 bias=neg_max[:],
-                accum_out=sums[:, c : c + 1],
+                accum_out=sums[:, i : i + 1],
             )
-            turned.append(psum.tile([P, 4, NQ], F32, name=f"turned{c}", tag=f"turned{c}"))
-            for t in range(4):
-                nc.tensor.transpose(turned[c][:, t, :], probs[:, t, :], ident[:])
-        nc.scalar.activation(sums[:, PAGES:], sink_col[:], ACT.Exp, bias=neg_max[:])
+            for t in range(first, end):
+                nc.tensor.transpose(turned[c][:, t, :], probs[:, t - first, :], ident[:])
+        nc.scalar.activation(sums[:, len(pieces) :], sink_col[:], ACT.Exp, bias=neg_max[:])
         total = keep.tile([P, 1], F32, name="total")
-        sums_again = keep.tile([P, PAGES + 1], F32, name="sums_again")
+        sums_again = keep.tile([P, len(pieces) + 1], F32, name="sums_again")
         nc.scalar.activation(sums_again[:], sums[:], ACT.Copy, accum_out=total[:])
 
         grouped, w_codes, w_plane = {}, {}, {}
@@ -184,7 +184,7 @@ def tile_attend_pkv4q_soft_sink_kernel(
             )
 
         def quantise(c):
-            behind = 49152 + 2048 * (c + 1)
+            behind = 49152 + 2048 * (c + 1) + 1024
             w_codes[c] = shared.tile([P, NQ], U32, name=f"w_codes{c}", align_bytes=64, offset=behind)
             w_plane[c] = shared.tile([P, NQ], U8, name=f"w_plane{c}", align_bytes=64, offset=behind + 512)
             nc.vector.quantize_mx(
@@ -197,7 +197,7 @@ def tile_attend_pkv4q_soft_sink_kernel(
         for c in range(last):
             weigh(c + 1)
             quantise(c)
-        inverse = shared.tile([P, 1], F32, name="inverse", offset=49152 + 2048 * last + 1024)
+        inverse = shared.tile([P, 1], F32, name="inverse", offset=49152 + 2048 * last + 1792)
         nc.vector.reciprocal(inverse[:], total[:])
         quantise(last)
 

@@ -151,7 +151,7 @@ def tile_attend_pkv4q_soft_sink_kernel(
 
         ident = shared.tile([P, P], F32, name="ident", offset=24576 + 2048 * (last - 1))
         make_identity(nc, ident[:])
-        pieces = [(c, 0, 4) for c in range(last)] + [(last, 0, 2), (last, 2, 4)]
+        pieces = [(0, 0, 2), (0, 2, 4), (1, 0, 4), (2, 0, 4), (last, 0, 2), (last, 2, 4)]
         sums = keep.tile([P, len(pieces) + 1], F32, name="sums")
         turned = [psum.tile([P, 4, NQ], F32, name=f"turned{c}", tag=f"turned{c}") for c in range(PAGES)]
         for i, (c, first, end) in enumerate(pieces):
@@ -177,9 +177,9 @@ def tile_attend_pkv4q_soft_sink_kernel(
         def weigh(c):
             grouped[c] = keep.tile([P, NQ, 4], BF16, name=f"grouped{c}", align_bytes=64)
             nc.vector.tensor_tensor(
-                grouped[c][:],
-                turned[c][:].rearrange("s t q -> s q t"),
-                token_columns[c][:].unsqueeze(1).to_broadcast([P, NQ, 4]),
+                grouped[c][:].rearrange("s (g i) t -> s g t i", i=4),
+                turned[c][:].rearrange("s t (g i) -> s g t i", i=4),
+                token_columns[c][:].unsqueeze(1).unsqueeze(3).to_broadcast([P, NQ // 4, 4, 4]),
                 ALU.mult,
             )
 

@@ -41,7 +41,7 @@ def tile_attend_pkv4q_soft_sink_kernel(
         key_scale_pool = key_scale_room[:, 64 : T + 64]
         nc.sync.dma_start(
             key_scale_pool.bitcast(I32)[0:32, :],
-            k_scales.rearrange("o f t -> (o f) t").bitcast(I32),
+            k_scales.rearrange("o f t -> f o t").bitcast(I32),
         )
         nc.sync.dma_start(key_list[:], offs)
         token_scale_pool = keep.tile([P, T], F32, name="token_scale_pool")
@@ -54,26 +54,25 @@ def tile_attend_pkv4q_soft_sink_kernel(
         nc.vector.memset(odd_run[32:64, :], 0)
         nc.vector.memset(odd_run[64:128, :], 0)
 
+        key_pool = keep.tile([P, T], I32, name="key_pool", align_bytes=64)
+        nc.sync.dma_start(key_pool[:], k_words[0].rearrange("p t b -> p (t b)").bitcast(I32))
         q_rows = q_scales[0].bitcast(I32).rearrange("o f q -> f o q")
         for j in range(4):
             nc.sync.dma_start(q_plane[:].bitcast(I32)[32 * j : 32 * j + 4, :, :], q_rows[4 * j : 4 * j + 4, :, :])
-        key_pool = keep.tile([P, T], I32, name="key_pool", align_bytes=64)
-        nc.sync.dma_start(key_pool[:], k_words[0].rearrange("p t b -> p (t b)").bitcast(I32))
         q_codes = keep.tile([P, PASSES, NQ], I32, name="q_codes", align_bytes=64)
         nc.sync.dma_start(q_codes[:], q_words[0].rearrange("o p q r -> p o (q r)").bitcast(I32))
         nc.sync.dma_start(value_list[:], voffs)
+        sink_col = keep.tile([P, 1], F32, name="sink_col")
+        nc.sync.dma_start(sink_col[:], sink[0])
 
-        key_scales_listed = keep.tile([P, N], U8, name="key_scales_listed")
+        key_scales_listed = shared.tile([P, N], U8, name="key_scales_listed", offset=12288)
         nc.vector.tensor_copy(key_scales_listed[:], key_scale_pool.indirect(key_list[:]))
         key_planes = shared.tile([P, PASSES * N], U8, name="key_planes", align_bytes=64, offset=T)
-        for o in reversed(range(PASSES)):
-            for j in (0, 2, 1, 3):
-                nc.sync.dma_start(
-                    key_planes[:].bitcast(I32)[32 * j : 32 * j + 4, o * N // 4 : (o + 1) * N // 4],
-                    key_scales_listed[:].bitcast(I32)[16 * o + 4 * j : 16 * o + 4 * (j + 1), :],
-                )
-        sink_col = shared.tile([P, 1], F32, name="sink_col", offset=2 * T)
-        nc.sync.dma_start(sink_col[:], sink[0])
+        for j in (0, 2, 1, 3):
+            nc.sync.dma_start(
+                key_planes[:].bitcast(I32)[32 * j : 32 * j + 4, :],
+                key_scales_listed[:].bitcast(I32)[8 * j : 8 * (j + 1), :],
+            )
         value_scale_pool = shared.tile([P, POOL_PAGES, DV], U8, name="value_scale_pool", offset=2 * T + 64)
         nc.gpsimd.memset(value_scale_pool[:].bitcast(I32), 0)
         v_rows = v_scales.bitcast(I32).rearrange("u f e -> f u e")
@@ -81,7 +80,7 @@ def tile_attend_pkv4q_soft_sink_kernel(
             nc.sync.dma_start(
                 value_scale_pool[:].bitcast(I32)[32 * j : 32 * j + 4, :, :], v_rows[4 * j : 4 * j + 4, :, :]
             )
-        value_pool = shared.tile([P, POOL_PAGES, DV], I32, name="value_pool", offset=0)
+        value_pool = shared.tile([P, POOL_PAGES, DV], I32, name="value_pool", offset=12288)
         nc.sync.dma_start(value_pool[:], v_words.rearrange("u p e r -> p u (e r)").bitcast(I32))
 
         def list_of(first, end):
@@ -97,10 +96,10 @@ def tile_attend_pkv4q_soft_sink_kernel(
                 nc.sync.dma_start(token_columns[c][:], row.rearrange("o (s t) -> o s t", t=4))
 
         last = PAGES - 1
-        token_scales_listed = keep.tile([P, N], F32, name="token_scales_listed")
-        gather_token_scales(token_scales_listed, 0, PAGES)
+        token_scales_listed = keep.tile([P, last * PAGE], F32, name="token_scales_listed")
+        gather_token_scales(token_scales_listed, 0, last)
 
-        maxima_room = shared.tile([P, 256], F32, name="maxima_room", offset=40960)
+        maxima_room = shared.tile([P, 32], F32, name="maxima_room", offset=40960)
         maxima = maxima_room[:, : PAGES + 1]
         nc.scalar.copy(maxima[:, PAGES:], sink_col[:])
 
@@ -137,21 +136,22 @@ def tile_attend_pkv4q_soft_sink_kernel(
             nc.vector.tensor_reduce(maxima[:, c : c + 1], scores[c][:], AX.X, ALU.max)
 
         value_scale_window = value_scale_pool[:].rearrange("p u e -> p (u e)")
-        first_plane = shared.tile([P, DV], U8, name="first_plane", align_bytes=64, offset=24576 + 2048 * last)
-        later_planes = shared.tile([P, last * DV], U8, name="later_planes", align_bytes=64, offset=41088)
+        first_plane = shared.tile([P, DV], U8, name="first_plane", align_bytes=64, offset=31744)
+        later_planes = shared.tile([P, last * DV], U8, name="later_planes", align_bytes=64, offset=49152 + 1024)
         value_planes = [first_plane[:]] + [later_planes[:, c * DV : (c + 1) * DV] for c in range(last)]
         neg_max = keep.tile([P, 1], F32, name="neg_max")
         nc.vector.tensor_copy(first_plane[:], value_scale_window.indirect(value_list[:, : DV // 16]))
         nc.vector.tensor_reduce(neg_max[:], maxima, AX.X, ALU.max, negate=True)
-        value_codes = shared.tile([P, PAGES * DV], U32, name="value_codes", align_bytes=64, offset=41536)
+        last_scales_listed = shared.tile([P, PAGE], F32, name="last_scales_listed", align_bytes=32, offset=40960 + 32 - 2048)
+        gather_token_scales(last_scales_listed, last, PAGES)
+        value_codes = shared.tile([P, PAGES * DV], U32, name="value_codes", align_bytes=64, offset=40960 + 64)
         nc.vector.tensor_copy(
             value_codes[:], value_pool[:].rearrange("p u e -> p (u e)").bitcast(U32).indirect(value_list[:])
         )
-        nc.vector.tensor_copy(later_planes[:], value_scale_window.indirect(value_list[:, DV // 16 :]))
 
         ident = shared.tile([P, P], F32, name="ident", offset=24576 + 2048 * (last - 1))
         make_identity(nc, ident[:])
-        pieces = [(0, 0, 2), (0, 2, 4), (1, 0, 4), (2, 0, 4), (last, 0, 2), (last, 2, 4)]
+        pieces = [(c, first, first + 2) for c in range(PAGES) for first in (0, 2)]
         sums = keep.tile([P, len(pieces) + 1], F32, name="sums")
         turned = [psum.tile([P, 4, NQ], F32, name=f"turned{c}", tag=f"turned{c}") for c in range(PAGES)]
         for i, (c, first, end) in enumerate(pieces):
@@ -194,6 +194,7 @@ def tile_attend_pkv4q_soft_sink_kernel(
             )
 
         weigh(0)
+        nc.vector.tensor_copy(later_planes[:], value_scale_window.indirect(value_list[:, DV // 16 :]))
         for c in range(last):
             weigh(c + 1)
             quantise(c)

@@ -1,7 +1,6 @@
 from contextlib import ExitStack
 
 import concourse.mybir as mybir
-from concourse.masks import make_identity
 
 N, T, D, DV, NQ = 2048, 4096, 1024, 128, 128
 P = 128
@@ -44,7 +43,7 @@ def tile_attend_pkv4q_soft_sink_kernel(
             k_scales.rearrange("o f t -> f o t").bitcast(I32),
         )
         nc.sync.dma_start(key_list[:], offs)
-        token_scale_pool = keep.tile([P, T], F32, name="token_scale_pool")
+        token_scale_pool = shared.tile([P, T], F32, name="token_scale_pool", offset=69632)
         nc.scalar.dma_start(token_scale_pool[P - 1 :, :], vs[0:1, :])
 
         q_plane = keep.tile([P, PASSES, NQ], U8, name="q_plane", align_bytes=64)
@@ -65,7 +64,7 @@ def tile_attend_pkv4q_soft_sink_kernel(
         sink_col = keep.tile([P, 1], F32, name="sink_col")
         nc.sync.dma_start(sink_col[:], sink[0])
 
-        key_scales_listed = shared.tile([P, N], U8, name="key_scales_listed", offset=12288)
+        key_scales_listed = keep.tile([P, N], U8, name="key_scales_listed")
         nc.vector.tensor_copy(key_scales_listed[:], key_scale_pool.indirect(key_list[:]))
         key_planes = shared.tile([P, PASSES * N], U8, name="key_planes", align_bytes=64, offset=T)
         for j in (0, 2, 1, 3):
@@ -80,28 +79,29 @@ def tile_attend_pkv4q_soft_sink_kernel(
             nc.sync.dma_start(
                 value_scale_pool[:].bitcast(I32)[32 * j : 32 * j + 4, :, :], v_rows[4 * j : 4 * j + 4, :, :]
             )
-        value_pool = shared.tile([P, POOL_PAGES, DV], I32, name="value_pool", offset=12288)
-        nc.sync.dma_start(value_pool[:], v_words.rearrange("u p e r -> p u (e r)").bitcast(I32))
 
         def list_of(first, end):
             return key_list[:, first * PAGE // 16 : end * PAGE // 16]
 
+        last = PAGES - 1
+        token_scales_listed = keep.tile([P, N], F32, name="token_scales_listed")
+        nc.vector.tensor_copy(token_scales_listed[:], token_scale_pool[:].indirect(key_list[:]))
         token_columns = {}
 
-        def gather_token_scales(listed, first, end):
-            nc.vector.tensor_copy(listed[:], token_scale_pool[:].indirect(list_of(first, end)))
-            for c in range(first, end):
-                token_columns[c] = keep.tile([P, 4], F32, name=f"token_columns{c}")
-                row = listed[P - 1 :, (c - first) * PAGE : (c - first + 1) * PAGE]
-                nc.sync.dma_start(token_columns[c][:], row.rearrange("o (s t) -> o s t", t=4))
+        def lay_out_token_scales(c):
+            token_columns[c] = keep.tile([P, 4], F32, name=f"token_columns{c}")
+            row = token_scales_listed[P - 1 :, c * PAGE : (c + 1) * PAGE]
+            nc.sync.dma_start(token_columns[c][:], row.rearrange("o (s t) -> o s t", t=4))
 
-        last = PAGES - 1
-        token_scales_listed = keep.tile([P, last * PAGE], F32, name="token_scales_listed")
-        gather_token_scales(token_scales_listed, 0, last)
+        lay_out_token_scales(0)
+        value_pool = shared.tile([P, POOL_PAGES, DV], I32, name="value_pool", offset=69632)
+        nc.sync.dma_start(value_pool[:], v_words.rearrange("u p e r -> p u (e r)").bitcast(I32))
+        for c in range(1, PAGES):
+            lay_out_token_scales(c)
 
         maxima_room = shared.tile([P, 32], F32, name="maxima_room", offset=40960)
         maxima = maxima_room[:, : PAGES + 1]
-        nc.scalar.copy(maxima[:, PAGES:], sink_col[:])
+        nc.scalar.mul(maxima[:, :1], sink_col[:], -1.0)
 
         key_pairs, scores = {}, {}
 
@@ -133,49 +133,87 @@ def tile_attend_pkv4q_soft_sink_kernel(
             score(c)
         score(last)
         for c in range(PAGES):
-            nc.vector.tensor_reduce(maxima[:, c : c + 1], scores[c][:], AX.X, ALU.max)
+            nc.vector.tensor_reduce(maxima[:, c + 1 : c + 2], scores[c][:], AX.X, ALU.max, negate=True)
+
+        distance = keep.tile([P, P], F32, name="distance")
+        nc.gpsimd.iota(distance[:], [[1, P]], base=0, channel_multiplier=-1, allow_small_or_imprecise_dtypes=True)
+        gap = keep.tile([P, P], F32, name="gap")
+        nc.scalar.activation(gap[:], distance[:], ACT.Abs)
+        ident = keep.tile([P, P], F32, name="ident")
+        nc.scalar.activation(ident[:], gap[:], ACT.Relu, bias=1.0, scale=-1.0)
+        early_sums = keep.tile([P, 2], F32, name="early_sums")
+        sums = keep.tile([P, 2 * PAGES + 2], F32, name="sums")
+        turned = [psum.tile([P, 4, NQ], F32, name=f"turned{c}", tag=f"turned{c}") for c in range(PAGES)]
+
+        def exponentials(c, half, bias, row_sum):
+            first = 2 * half
+            probs = shared.tile(
+                [P, 2, P], F32, name=f"probs{c}_{half}", align_bytes=64, offset=49152 + 2048 * c + 512 * first
+            )
+            nc.scalar.activation(
+                probs[:].rearrange("q t s -> q s t"),
+                scores[c][:].rearrange("q (s t) -> q s t", t=4)[:, :, first : first + 2],
+                ACT.Exp,
+                bias=bias,
+                accum_out=row_sum,
+            )
+            for t in range(2):
+                nc.tensor.transpose(turned[c][:, first + t, :], probs[:, t, :], ident[:])
+
+        for half in range(2):
+            exponentials(0, half, maxima[:, 1:2], early_sums[:, half : half + 1])
+        early_logits = keep.tile([P, 2], F32, name="early_logits")
+        nc.scalar.copy(early_logits[:], maxima[:, :2])
+        early_scaled = keep.tile([P, 4, NQ], F32, name="early_scaled", align_bytes=64)
+        early_back = psum.tile([P, 4, P], F32, name="early_back", tag="scores0")
+        for t in range(4):
+            nc.scalar.activation(
+                early_scaled[:, t, :], turned[0][:, t, :], ACT.Copy, scale=token_columns[0][:, t : t + 1]
+            )
+            nc.tensor.transpose(early_back[:, t, :], early_scaled[:, t, :], ident[:])
 
         value_scale_window = value_scale_pool[:].rearrange("p u e -> p (u e)")
         first_plane = shared.tile([P, DV], U8, name="first_plane", align_bytes=64, offset=31744)
-        later_planes = shared.tile([P, last * DV], U8, name="later_planes", align_bytes=64, offset=49152 + 1024)
+        later_planes = shared.tile([P, last * DV], U8, name="later_planes", align_bytes=64, offset=40960 + 64 - 384)
         value_planes = [first_plane[:]] + [later_planes[:, c * DV : (c + 1) * DV] for c in range(last)]
         neg_max = keep.tile([P, 1], F32, name="neg_max")
         nc.vector.tensor_copy(first_plane[:], value_scale_window.indirect(value_list[:, : DV // 16]))
-        nc.vector.tensor_reduce(neg_max[:], maxima, AX.X, ALU.max, negate=True)
-        last_scales_listed = shared.tile([P, PAGE], F32, name="last_scales_listed", align_bytes=32, offset=40960 + 32 - 2048)
-        gather_token_scales(last_scales_listed, last, PAGES)
+        nc.vector.tensor_reduce(neg_max[:], maxima, AX.X, ALU.min)
         value_codes = shared.tile([P, PAGES * DV], U32, name="value_codes", align_bytes=64, offset=40960 + 64)
         nc.vector.tensor_copy(
             value_codes[:], value_pool[:].rearrange("p u e -> p (u e)").bitcast(U32).indirect(value_list[:])
         )
+        nc.vector.tensor_copy(later_planes[:], value_scale_window.indirect(value_list[:, DV // 16 :]))
 
-        ident = shared.tile([P, P], F32, name="ident", offset=24576 + 2048 * (last - 1))
-        make_identity(nc, ident[:])
-        pieces = [(c, first, first + 2) for c in range(PAGES) for first in (0, 2)]
-        sums = keep.tile([P, len(pieces) + 1], F32, name="sums")
-        turned = [psum.tile([P, 4, NQ], F32, name=f"turned{c}", tag=f"turned{c}") for c in range(PAGES)]
-        for i, (c, first, end) in enumerate(pieces):
-            probs = shared.tile(
-                [P, end - first, P], F32, name=f"probs{i}", align_bytes=64, offset=49152 + 2048 * c + 512 * first
-            )
-            nc.scalar.activation(
-                probs[:].rearrange("q t s -> q s t"),
-                scores[c][:].rearrange("q (s t) -> q s t", t=4)[:, :, first:end],
-                ACT.Exp,
-                bias=neg_max[:],
-                accum_out=sums[:, i : i + 1],
-            )
-            for t in range(first, end):
-                nc.tensor.transpose(turned[c][:, t, :], probs[:, t - first, :], ident[:])
-        nc.scalar.activation(sums[:, len(pieces) :], sink_col[:], ACT.Exp, bias=neg_max[:])
-        total = keep.tile([P, 1], F32, name="total")
-        sums_again = keep.tile([P, len(pieces) + 1], F32, name="sums_again")
-        nc.scalar.activation(sums_again[:], sums[:], ACT.Copy, accum_out=total[:])
+        factors = sums[:, 2 * PAGES :]
+        for c in range(1, PAGES):
+            for half in range(2):
+                exponentials(c, half, neg_max[:], sums[:, 2 * c + half : 2 * c + half + 1])
+            if c == 1:
+                nc.scalar.activation(factors, early_logits[:], ACT.Exp, bias=neg_max[:], scale=-1.0)
 
         grouped, w_codes, w_plane = {}, {}, {}
+        for c in range(PAGES):
+            grouped[c] = shared.tile([P, NQ, 4], BF16, name=f"grouped{c}", align_bytes=64, offset=61440 + 1024 * c)
+
+        early_pairs = keep.tile([P, 2, P, 2], BF16, name="early_pairs", align_bytes=64)
+        back_pairs = early_back[:].rearrange("q (u e) s -> q u s e", e=2)
+        nc.vector.tensor_scalar(early_pairs[:, 0, :, :], back_pairs[:, 0, :, :], factors[:, 1:2], None, ALU.mult)
+        nc.scalar.activation(early_pairs[:, 1, :, :], back_pairs[:, 1, :, :], ACT.Copy, scale=factors[:, 1:2])
+        early_words = psum.tile([P, 2, NQ], F32, name="early_words", tag="turned0")
+        for u in range(2):
+            words = early_pairs[:, u, :, :].rearrange("q s e -> q (s e)").bitcast(F32)
+            nc.tensor.transpose(early_words[:, u, :], words, ident[:])
+        nc.scalar.activation(sums[:, :2], early_sums[:], ACT.Copy, scale=factors[:, 1:2])
+        total = keep.tile([P, 1], F32, name="total")
+        sums_again = keep.tile([P, 2 * PAGES + 1], F32, name="sums_again")
+        nc.scalar.activation(sums_again[:], sums[:, : 2 * PAGES + 1], ACT.Copy, accum_out=total[:])
+        nc.scalar.copy(
+            grouped[0][:].rearrange("s q t -> s (q t)").bitcast(F32).rearrange("s (q u) -> s q u", u=2),
+            early_words[:].rearrange("s u q -> s q u"),
+        )
 
         def weigh(c):
-            grouped[c] = keep.tile([P, NQ, 4], BF16, name=f"grouped{c}", align_bytes=64)
             nc.vector.tensor_tensor(
                 grouped[c][:].rearrange("s (g i) t -> s g t i", i=4),
                 turned[c][:].rearrange("s t (g i) -> s g t i", i=4),
@@ -183,35 +221,35 @@ def tile_attend_pkv4q_soft_sink_kernel(
                 ALU.mult,
             )
 
-        def quantise(c):
-            behind = 49152 + 2048 * (c + 1) + 1024
-            w_codes[c] = shared.tile([P, NQ], U32, name=f"w_codes{c}", align_bytes=64, offset=behind)
-            w_plane[c] = shared.tile([P, NQ], U8, name=f"w_plane{c}", align_bytes=64, offset=behind + 512)
+        def quantise(c, offset):
+            w_codes[c] = shared.tile([P, NQ], U32, name=f"w_codes{c}", align_bytes=64, offset=offset)
+            w_plane[c] = shared.tile([P, NQ], U8, name=f"w_plane{c}", align_bytes=64, offset=offset + 512)
             nc.vector.quantize_mx(
                 out=w_codes[c][:].bitcast(FP8X4),
                 scales=w_plane[c][:],
                 in_=grouped[c][:].rearrange("p q t -> p (q t)"),
             )
 
-        weigh(0)
-        nc.vector.tensor_copy(later_planes[:], value_scale_window.indirect(value_list[:, DV // 16 :]))
-        for c in range(last):
+        weigh(1)
+        for c in range(1, last):
             weigh(c + 1)
-            quantise(c)
-        inverse = shared.tile([P, 1], F32, name="inverse", offset=49152 + 2048 * last + 1792)
+            quantise(c, 49152 + 2048 * (c + 1) + 1024)
+        quantise(0, 49152)
+        quantise(last, 49152 + 2048 * PAGES)
+        inverse = shared.tile([P, 1], F32, name="inverse", offset=61440 + 1024 * last)
         nc.vector.reciprocal(inverse[:], total[:])
-        quantise(last)
 
-        acc = psum.tile([P, DV], F32, name="acc", tag="turned2")
-        for c in range(PAGES):
+        acc = psum.tile([P, DV], F32, name="acc", tag="scores0")
+        order = (1, 2, 0, last)
+        for c in order:
             nc.tensor.matmul_mx(
                 out=acc[:],
                 lhsT=w_codes[c][:].bitcast(FP8X4),
                 lhsT_scale=w_plane[c][:],
                 rhs=value_codes[:, c * DV : (c + 1) * DV].bitcast(FP8X4),
                 rhs_scale=value_planes[c],
-                start=(c == 0),
-                stop=(c == last),
+                start=(c == order[0]),
+                stop=(c == order[-1]),
             )
 
         result = keep.tile([P, DV], F32, name="result")

@@ -84,13 +84,15 @@ def tile_attend_pkv4q_soft_sink_kernel(
             return key_list[:, first * PAGE // 16 : end * PAGE // 16]
 
         last = PAGES - 1
-        token_scales_listed = keep.tile([P, N], F32, name="token_scales_listed")
-        nc.vector.tensor_copy(token_scales_listed[:], token_scale_pool[:].indirect(key_list[:]))
+        first_listed = keep.tile([P, N // 2], F32, name="first_listed")
+        nc.vector.tensor_copy(first_listed[:], token_scale_pool[:].indirect(list_of(0, 2)))
+        second_listed = keep.tile([P, N // 2], F32, name="second_listed")
+        nc.scalar.activation(second_listed[:], token_scale_pool[:].indirect(list_of(2, 4)), ACT.Copy)
         token_columns = {}
 
         def lay_out_token_scales(c):
             token_columns[c] = keep.tile([P, 4], F32, name=f"token_columns{c}")
-            row = token_scales_listed[P - 1 :, c * PAGE : (c + 1) * PAGE]
+            row = (first_listed, second_listed)[c // 2][P - 1 :, c % 2 * PAGE : (c % 2 + 1) * PAGE]
             nc.sync.dma_start(token_columns[c][:], row.rearrange("o (s t) -> o s t", t=4))
 
         lay_out_token_scales(0)

@@ -47,7 +47,6 @@ def tile_attend_pkv4q_soft_sink_kernel(
         nc.scalar.dma_start(token_scale_pool[P - 1 :, :], vs[0:1, :])
 
         q_plane = keep.tile([P, PASSES, NQ], U8, name="q_plane", align_bytes=64)
-        nc.gpsimd.memset(q_plane[:].bitcast(I32), 0)
         nc.gpsimd.memset(token_scale_pool[:].bitcast(I32)[: P - 1, :], 0)
         odd_run = key_scale_room[:, 60 : T + 64].bitcast(I32)
         nc.vector.memset(odd_run[32:64, :], 0)
@@ -101,9 +100,9 @@ def tile_attend_pkv4q_soft_sink_kernel(
         for c in range(1, PAGES):
             lay_out_token_scales(c)
 
-        maxima_room = shared.tile([P, 32], F32, name="maxima_room", offset=40960)
-        maxima = maxima_room[:, : PAGES + 1]
-        nc.scalar.mul(maxima[:, :1], sink_col[:], -1.0)
+        maxima = shared.tile([P, PAGES], F32, name="maxima", offset=36864)
+        neg_sink = shared.tile([P, 1], F32, name="neg_sink", offset=40960)
+        nc.scalar.mul(neg_sink[:], sink_col[:], -1.0)
 
         key_pairs, scores = {}, {}
 
@@ -134,8 +133,12 @@ def tile_attend_pkv4q_soft_sink_kernel(
             gather_keys(c + 1)
             score(c)
         score(last)
-        for c in range(PAGES):
-            nc.vector.tensor_reduce(maxima[:, c + 1 : c + 2], scores[c][:], AX.X, ALU.max, negate=True)
+        for c in range(last):
+            nc.vector.tensor_reduce(maxima[:, c : c + 1], scores[c][:], AX.X, ALU.max, negate=True)
+        negated = keep.tile([P, PAGE], F32, name="negated")
+        nc.vector.tensor_scalar(
+            negated[:], scores[last][:], -1.0, neg_sink[:], ALU.mult, ALU.min, accum_out=maxima[:, last:]
+        )
 
         distance = keep.tile([P, P], F32, name="distance")
         nc.gpsimd.iota(distance[:], [[1, P]], base=0, channel_multiplier=-1, allow_small_or_imprecise_dtypes=True)
@@ -143,29 +146,36 @@ def tile_attend_pkv4q_soft_sink_kernel(
         nc.scalar.activation(gap[:], distance[:], ACT.Abs)
         ident = keep.tile([P, P], F32, name="ident")
         nc.scalar.activation(ident[:], gap[:], ACT.Relu, bias=1.0, scale=-1.0)
-        early_sums = keep.tile([P, 2], F32, name="early_sums")
-        sums = keep.tile([P, 2 * PAGES + 2], F32, name="sums")
-        turned = [psum.tile([P, 4, NQ], F32, name=f"turned{c}", tag=f"turned{c}") for c in range(PAGES)]
+        early_sums = keep.tile([P, 4], F32, name="early_sums")
+        sums = keep.tile([P, 2 * PAGES + 1], F32, name="sums")
+        turned = {c: psum.tile([P, 4, NQ], F32, name=f"turned{c}", tag=f"turned{c}") for c in (0, 2, 3)}
 
-        def exponentials(c, half, bias, row_sum):
-            first = 2 * half
-            probs = shared.tile(
-                [P, 2, P], F32, name=f"probs{c}_{half}", align_bytes=64, offset=49152 + 2048 * c + 512 * first
-            )
+        def exponential(probs, c, half, bias, row_sum):
+            logits, sign = (negated, -1.0) if c == last else (scores[c], 1.0)
             nc.scalar.activation(
-                probs[:].rearrange("q t s -> q s t"),
-                scores[c][:].rearrange("q (s t) -> q s t", t=4)[:, :, first : first + 2],
+                probs.rearrange("q t s -> q s t"),
+                logits[:].rearrange("q (s t) -> q s t", t=4)[:, :, 2 * half : 2 * half + 2],
                 ACT.Exp,
                 bias=bias,
+                scale=sign,
                 accum_out=row_sum,
             )
+
+        def exponentials(c, half, bias, row_sum):
+            probs = shared.tile(
+                [P, 2, P], F32, name=f"probs{c}_{half}", align_bytes=64, offset=49152 + 2048 * c + 1024 * half
+            )
+            exponential(probs[:], c, half, bias, row_sum)
             for t in range(2):
-                nc.tensor.transpose(turned[c][:, first + t, :], probs[:, t, :], ident[:])
+                nc.tensor.transpose(turned[c][:, 2 * half + t, :], probs[:, t, :], ident[:])
 
         for half in range(2):
-            exponentials(0, half, maxima[:, 1:2], early_sums[:, half : half + 1])
-        early_logits = keep.tile([P, 2], F32, name="early_logits")
-        nc.scalar.copy(early_logits[:], maxima[:, :2])
+            exponentials(0, half, maxima[:, 0:1], early_sums[:, half : half + 1])
+        second_probs = keep.tile([P, 4, P], F32, name="second_probs", align_bytes=64)
+        for half in range(2):
+            exponential(
+                second_probs[:, 2 * half : 2 * half + 2, :], 1, half, maxima[:, 1:2], early_sums[:, 2 + half : 3 + half]
+            )
         early_scaled = keep.tile([P, 4, NQ], F32, name="early_scaled", align_bytes=64)
         early_back = psum.tile([P, 4, P], F32, name="early_back", tag="scores0")
         for t in range(4):
@@ -176,23 +186,28 @@ def tile_attend_pkv4q_soft_sink_kernel(
 
         value_scale_window = value_scale_pool[:].rearrange("p u e -> p (u e)")
         first_plane = shared.tile([P, DV], U8, name="first_plane", align_bytes=64, offset=31744)
-        later_planes = shared.tile([P, last * DV], U8, name="later_planes", align_bytes=64, offset=40960 + 64 - 384)
+        later_planes = shared.tile([P, last * DV], U8, name="later_planes", align_bytes=64, offset=40960)
         value_planes = [first_plane[:]] + [later_planes[:, c * DV : (c + 1) * DV] for c in range(last)]
         neg_max = keep.tile([P, 1], F32, name="neg_max")
         nc.vector.tensor_copy(first_plane[:], value_scale_window.indirect(value_list[:, : DV // 16]))
-        nc.vector.tensor_reduce(neg_max[:], maxima, AX.X, ALU.min)
-        value_codes = shared.tile([P, PAGES * DV], U32, name="value_codes", align_bytes=64, offset=40960 + 64)
+        nc.vector.tensor_reduce(neg_max[:], maxima[:], AX.X, ALU.min)
+        nc.vector.tensor_copy(later_planes[:], value_scale_window.indirect(value_list[:, DV // 16 :]))
+        factors = keep.tile([P, 2], F32, name="factors")
+        nc.scalar.activation(factors[:], maxima[:, :2], ACT.Exp, bias=neg_max[:], scale=-1.0)
+        second_scaled = shared.tile([P, 4, P], F32, name="second_scaled", align_bytes=64, offset=49152 + 2048)
+        nc.vector.tensor_scalar(second_scaled[:], second_probs[:], factors[:, 1:2], None, ALU.mult)
+        value_codes = shared.tile([P, PAGES * DV], U32, name="value_codes", align_bytes=64, offset=36864)
         nc.vector.tensor_copy(
             value_codes[:], value_pool[:].rearrange("p u e -> p (u e)").bitcast(U32).indirect(value_list[:])
         )
-        nc.vector.tensor_copy(later_planes[:], value_scale_window.indirect(value_list[:, DV // 16 :]))
 
-        factors = sums[:, 2 * PAGES :]
-        for c in range(1, PAGES):
-            for half in range(2):
-                exponentials(c, half, neg_max[:], sums[:, 2 * c + half : 2 * c + half + 1])
-            if c == 1:
-                nc.scalar.activation(factors, early_logits[:], ACT.Exp, bias=neg_max[:], scale=-1.0)
+        for half in range(2):
+            exponentials(2, half, neg_max[:], sums[:, 4 + half : 5 + half])
+        turned[1] = psum.tile([P, 4, NQ], F32, name="turned1", tag="scores2")
+        for t in range(4):
+            nc.tensor.transpose(turned[1][:, t, :], second_scaled[:, t, :], ident[:])
+        for half in range(2):
+            exponentials(last, half, neg_max[:], sums[:, 6 + half : 7 + half])
 
         grouped, w_codes, w_plane = {}, {}, {}
         for c in range(PAGES):
@@ -200,16 +215,19 @@ def tile_attend_pkv4q_soft_sink_kernel(
 
         early_pairs = keep.tile([P, 2, P, 2], BF16, name="early_pairs", align_bytes=64)
         back_pairs = early_back[:].rearrange("q (u e) s -> q u s e", e=2)
-        nc.vector.tensor_scalar(early_pairs[:, 0, :, :], back_pairs[:, 0, :, :], factors[:, 1:2], None, ALU.mult)
-        nc.scalar.activation(early_pairs[:, 1, :, :], back_pairs[:, 1, :, :], ACT.Copy, scale=factors[:, 1:2])
         early_words = psum.tile([P, 2, NQ], F32, name="early_words", tag="turned0")
         for u in range(2):
+            nc.scalar.activation(early_pairs[:, u, :, :], back_pairs[:, u, :, :], ACT.Copy, scale=factors[:, 0:1])
             words = early_pairs[:, u, :, :].rearrange("q s e -> q (s e)").bitcast(F32)
             nc.tensor.transpose(early_words[:, u, :], words, ident[:])
-        nc.scalar.activation(sums[:, :2], early_sums[:], ACT.Copy, scale=factors[:, 1:2])
+        for c in range(2):
+            nc.scalar.activation(
+                sums[:, 2 * c : 2 * c + 2], early_sums[:, 2 * c : 2 * c + 2], ACT.Copy, scale=factors[:, c : c + 1]
+            )
+        nc.scalar.activation(sums[:, 2 * PAGES :], sink_col[:], ACT.Exp, bias=neg_max[:])
         total = keep.tile([P, 1], F32, name="total")
         sums_again = keep.tile([P, 2 * PAGES + 1], F32, name="sums_again")
-        nc.scalar.activation(sums_again[:], sums[:, : 2 * PAGES + 1], ACT.Copy, accum_out=total[:])
+        nc.scalar.activation(sums_again[:], sums[:], ACT.Copy, accum_out=total[:])
         nc.scalar.copy(
             grouped[0][:].rearrange("s q t -> s (q t)").bitcast(F32).rearrange("s (q u) -> s q u", u=2),
             early_words[:].rearrange("s u q -> s q u"),
@@ -232,17 +250,18 @@ def tile_attend_pkv4q_soft_sink_kernel(
                 in_=grouped[c][:].rearrange("p q t -> p (q t)"),
             )
 
+        weigh(2)
         weigh(1)
-        for c in range(1, last):
-            weigh(c + 1)
-            quantise(c, 49152 + 2048 * (c + 1) + 1024)
+        quantise(2, 49152 + 2048)
+        weigh(last)
+        quantise(1, 49152 + 2048 * last + 1024)
         quantise(0, 49152)
         quantise(last, 49152 + 2048 * PAGES)
         inverse = shared.tile([P, 1], F32, name="inverse", offset=61440 + 1024 * last)
         nc.vector.reciprocal(inverse[:], total[:])
 
         acc = psum.tile([P, DV], F32, name="acc", tag="scores0")
-        order = (1, 2, 0, last)
+        order = (2, 1, 0, last)
         for c in order:
             nc.tensor.matmul_mx(
                 out=acc[:],

@@ -95,9 +95,10 @@ def tile_attend_pkv4q_soft_sink_kernel(
             nc.sync.dma_start(token_columns[c][:], row.rearrange("o (s t) -> o s t", t=4))
 
         lay_out_token_scales(0)
+        lay_out_token_scales(1)
         value_pool = shared.tile([P, POOL_PAGES, DV], I32, name="value_pool", offset=69632)
         nc.sync.dma_start(value_pool[:], v_words.rearrange("u p e r -> p u (e r)").bitcast(I32))
-        for c in range(1, PAGES):
+        for c in range(2, PAGES):
             lay_out_token_scales(c)
 
         maxima = shared.tile([P, PAGES], F32, name="maxima", offset=36864)
@@ -153,7 +154,7 @@ def tile_attend_pkv4q_soft_sink_kernel(
         def exponential(probs, c, half, bias, row_sum):
             logits, sign = (negated, -1.0) if c == last else (scores[c], 1.0)
             nc.scalar.activation(
-                probs.rearrange("q t s -> q s t"),
+                probs,
                 logits[:].rearrange("q (s t) -> q s t", t=4)[:, :, 2 * half : 2 * half + 2],
                 ACT.Exp,
                 bias=bias,
@@ -165,17 +166,18 @@ def tile_attend_pkv4q_soft_sink_kernel(
             probs = shared.tile(
                 [P, 2, P], F32, name=f"probs{c}_{half}", align_bytes=64, offset=49152 + 2048 * c + 1024 * half
             )
-            exponential(probs[:], c, half, bias, row_sum)
+            exponential(probs[:].rearrange("q t s -> q s t"), c, half, bias, row_sum)
             for t in range(2):
                 nc.tensor.transpose(turned[c][:, 2 * half + t, :], probs[:, t, :], ident[:])
 
         for half in range(2):
             exponentials(0, half, maxima[:, 0:1], early_sums[:, half : half + 1])
-        second_probs = keep.tile([P, 4, P], F32, name="second_probs", align_bytes=64)
+        second_probs = keep.tile([P, 2, P, 2], F32, name="second_probs", align_bytes=64)
         for half in range(2):
-            exponential(
-                second_probs[:, 2 * half : 2 * half + 2, :], 1, half, maxima[:, 1:2], early_sums[:, 2 + half : 3 + half]
-            )
+            exponential(second_probs[:, half, :, :], 1, half, maxima[:, 1:2], early_sums[:, 2 + half : 3 + half])
+        spread = psum.tile([P, 4, P], F32, name="spread", tag="scores1")
+        for t in range(4):
+            nc.tensor.transpose(spread[:, t, :], token_columns[1][:, t : t + 1].to_broadcast([P, P]), ident[:])
         early_scaled = keep.tile([P, 4, NQ], F32, name="early_scaled", align_bytes=64)
         early_back = psum.tile([P, 4, P], F32, name="early_back", tag="scores0")
         for t in range(4):
@@ -194,8 +196,16 @@ def tile_attend_pkv4q_soft_sink_kernel(
         nc.vector.tensor_copy(later_planes[:], value_scale_window.indirect(value_list[:, DV // 16 :]))
         factors = keep.tile([P, 2], F32, name="factors")
         nc.scalar.activation(factors[:], maxima[:, :2], ACT.Exp, bias=neg_max[:], scale=-1.0)
-        second_scaled = shared.tile([P, 4, P], F32, name="second_scaled", align_bytes=64, offset=49152 + 2048)
-        nc.vector.tensor_scalar(second_scaled[:], second_probs[:], factors[:, 1:2], None, ALU.mult)
+        second_pairs = keep.tile([P, 2, P, 2], BF16, name="second_pairs", align_bytes=64)
+        for u in range(2):
+            nc.vector.scalar_tensor_tensor(
+                second_pairs[:, u, :, :],
+                second_probs[:, u, :, :],
+                factors[:, 1:2],
+                spread[:, 2 * u : 2 * u + 2, :].rearrange("q e s -> q s e"),
+                ALU.mult,
+                ALU.mult,
+            )
         value_codes = shared.tile([P, PAGES * DV], U32, name="value_codes", align_bytes=64, offset=36864)
         nc.vector.tensor_copy(
             value_codes[:], value_pool[:].rearrange("p u e -> p (u e)").bitcast(U32).indirect(value_list[:])
@@ -203,11 +213,12 @@ def tile_attend_pkv4q_soft_sink_kernel(
 
         for half in range(2):
             exponentials(2, half, neg_max[:], sums[:, 4 + half : 5 + half])
-        turned[1] = psum.tile([P, 4, NQ], F32, name="turned1", tag="scores2")
-        for t in range(4):
-            nc.tensor.transpose(turned[1][:, t, :], second_scaled[:, t, :], ident[:])
         for half in range(2):
             exponentials(last, half, neg_max[:], sums[:, 6 + half : 7 + half])
+        second_words = psum.tile([P, 2, NQ], F32, name="second_words", tag="scores2")
+        for u in range(2):
+            words = second_pairs[:, u, :, :].rearrange("q s e -> q (s e)").bitcast(F32)
+            nc.tensor.transpose(second_words[:, u, :], words, ident[:])
 
         grouped, w_codes, w_plane = {}, {}, {}
         for c in range(PAGES):
@@ -220,6 +231,14 @@ def tile_attend_pkv4q_soft_sink_kernel(
             nc.scalar.activation(early_pairs[:, u, :, :], back_pairs[:, u, :, :], ACT.Copy, scale=factors[:, 0:1])
             words = early_pairs[:, u, :, :].rearrange("q s e -> q (s e)").bitcast(F32)
             nc.tensor.transpose(early_words[:, u, :], words, ident[:])
+
+        def copy_words(c, words):
+            nc.scalar.copy(
+                grouped[c][:].rearrange("s q t -> s (q t)").bitcast(F32).rearrange("s (q u) -> s q u", u=2),
+                words[:].rearrange("s u q -> s q u"),
+            )
+
+        copy_words(1, second_words)
         for c in range(2):
             nc.scalar.activation(
                 sums[:, 2 * c : 2 * c + 2], early_sums[:, 2 * c : 2 * c + 2], ACT.Copy, scale=factors[:, c : c + 1]
@@ -228,10 +247,7 @@ def tile_attend_pkv4q_soft_sink_kernel(
         total = keep.tile([P, 1], F32, name="total")
         sums_again = keep.tile([P, 2 * PAGES + 1], F32, name="sums_again")
         nc.scalar.activation(sums_again[:], sums[:], ACT.Copy, accum_out=total[:])
-        nc.scalar.copy(
-            grouped[0][:].rearrange("s q t -> s (q t)").bitcast(F32).rearrange("s (q u) -> s q u", u=2),
-            early_words[:].rearrange("s u q -> s q u"),
-        )
+        copy_words(0, early_words)
 
         def weigh(c):
             nc.vector.tensor_tensor(
@@ -251,12 +267,11 @@ def tile_attend_pkv4q_soft_sink_kernel(
             )
 
         weigh(2)
-        weigh(1)
-        quantise(2, 49152 + 2048)
         weigh(last)
-        quantise(1, 49152 + 2048 * last + 1024)
+        quantise(2, 49152 + 2048 * last + 1024)
+        quantise(1, 49152 + 2048 * PAGES - 64)
         quantise(0, 49152)
-        quantise(last, 49152 + 2048 * PAGES)
+        quantise(last, 49152 + 2048 * PAGES + 1024)
         inverse = shared.tile([P, 1], F32, name="inverse", offset=61440 + 1024 * last)
         nc.vector.reciprocal(inverse[:], total[:])
 

from contextlib import ExitStack

import concourse.mybir as mybir

N, T, D, DV, NQ = 2048, 4096, 1024, 128, 128
P = 128
PAGE = 512
PAGES = N // PAGE
POOL_PAGES = T // PAGE
PASSES = D // 512

FLOPS = 2 * NQ * N * (D + DV)

F32 = mybir.dt.float32
BF16 = mybir.dt.bfloat16
I32 = mybir.dt.int32
U32 = mybir.dt.uint32
U16 = mybir.dt.uint16
U8 = mybir.dt.uint8
FP8X4 = mybir.dt.float8_e4m3fn_x4
FP4X4 = mybir.dt.float4_e2m1fn_x4
ALU = mybir.AluOpType
ACT = mybir.ActivationFunctionType
AX = mybir.AxisListType


def tile_attend_pkv4q_soft_sink_kernel(
    tc, q_words, q_scales, k_words, k_scales, v_words, v_scales, vs, sink, offs, voffs, out
):
    nc = tc.nc
    with ExitStack() as ctx:
        lists = ctx.enter_context(tc.tile_pool(name="lists", bufs=1))
        keep = ctx.enter_context(tc.tile_pool(name="keep", bufs=1))
        shared = ctx.enter_context(tc.tile_pool(name="shared", bufs=1))
        psum = ctx.enter_context(tc.psum_pool(name="psum", bufs=1))

        key_list = lists.tile([P, N // 16], U16, name="key_list")
        value_list = lists.tile([P, PAGES * DV // 16], U16, name="value_list")
        key_scale_room = shared.tile([P, T + 192], U8, name="key_scale_room", align_bytes=64, offset=T - 64)
        key_scale_pool = key_scale_room[:, 64 : T + 64]
        nc.sync.dma_start(
            key_scale_pool.bitcast(I32)[0:32, :],
            k_scales.rearrange("o f t -> f o t").bitcast(I32),
        )
        nc.sync.dma_start(key_list[:], offs)
        token_scale_pool = shared.tile([P, T], F32, name="token_scale_pool", offset=69632)
        nc.scalar.dma_start(token_scale_pool[P - 1 :, :], vs[0:1, :])

        q_plane = keep.tile([P, PASSES, NQ], U8, name="q_plane", align_bytes=64)
        nc.gpsimd.memset(token_scale_pool[:].bitcast(I32)[: P - 1, :], 0)
        odd_run = key_scale_room[:, 60 : T + 64].bitcast(I32)
        nc.vector.memset(odd_run[32:64, :], 0)
        nc.vector.memset(odd_run[64:128, :], 0)

        key_pool = keep.tile([P, T], I32, name="key_pool", align_bytes=64)
        nc.sync.dma_start(key_pool[:], k_words[0].rearrange("p t b -> p (t b)").bitcast(I32))
        q_rows = q_scales[0].bitcast(I32).rearrange("o f q -> f o q")
        for j in range(4):
            nc.sync.dma_start(q_plane[:].bitcast(I32)[32 * j : 32 * j + 4, :, :], q_rows[4 * j : 4 * j + 4, :, :])
        q_codes = keep.tile([P, PASSES, NQ], I32, name="q_codes", align_bytes=64)
        nc.sync.dma_start(q_codes[:], q_words[0].rearrange("o p q r -> p o (q r)").bitcast(I32))
        nc.sync.dma_start(value_list[:], voffs)
        sink_col = keep.tile([P, 1], F32, name="sink_col")
        nc.sync.dma_start(sink_col[:], sink[0])

        key_scales_listed = keep.tile([P, N], U8, name="key_scales_listed")
        nc.vector.tensor_copy(key_scales_listed[:], key_scale_pool.indirect(key_list[:]))
        key_planes = shared.tile([P, PASSES * N], U8, name="key_planes", align_bytes=64, offset=T)
        for j in (0, 2, 1, 3):
            nc.sync.dma_start(
                key_planes[:].bitcast(I32)[32 * j : 32 * j + 4, :],
                key_scales_listed[:].bitcast(I32)[8 * j : 8 * (j + 1), :],
            )
        value_scale_pool = shared.tile([P, POOL_PAGES, DV], U8, name="value_scale_pool", offset=2 * T + 64)
        nc.gpsimd.memset(value_scale_pool[:].bitcast(I32), 0)
        v_rows = v_scales.bitcast(I32).rearrange("u f e -> f u e")
        for j in range(4):
            nc.sync.dma_start(
                value_scale_pool[:].bitcast(I32)[32 * j : 32 * j + 4, :, :], v_rows[4 * j : 4 * j + 4, :, :]
            )

        def list_of(first, end):
            return key_list[:, first * PAGE // 16 : end * PAGE // 16]

        last = PAGES - 1
        first_listed = keep.tile([P, N // 2], F32, name="first_listed")
        nc.vector.tensor_copy(first_listed[:], token_scale_pool[:].indirect(list_of(0, 2)))
        second_listed = keep.tile([P, N // 2], F32, name="second_listed")
        nc.scalar.activation(second_listed[:], token_scale_pool[:].indirect(list_of(2, 4)), ACT.Copy)
        token_columns = {}

        def lay_out_token_scales(c):
            token_columns[c] = keep.tile([P, 4], F32, name=f"token_columns{c}")
            row = (first_listed, second_listed)[c // 2][P - 1 :, c % 2 * PAGE : (c % 2 + 1) * PAGE]
            nc.sync.dma_start(token_columns[c][:], row.rearrange("o (s t) -> o s t", t=4))

        lay_out_token_scales(0)
        lay_out_token_scales(1)
        value_pool = shared.tile([P, POOL_PAGES, DV], I32, name="value_pool", offset=69632)
        nc.sync.dma_start(value_pool[:], v_words.rearrange("u p e r -> p u (e r)").bitcast(I32))
        for c in range(2, PAGES):
            lay_out_token_scales(c)

        maxima = shared.tile([P, PAGES], F32, name="maxima", offset=36864)
        neg_sink = shared.tile([P, 1], F32, name="neg_sink", offset=40960)
        nc.scalar.mul(neg_sink[:], sink_col[:], -1.0)

        key_pairs, scores = {}, {}

        def gather_keys(c):
            key_pairs[c] = keep.tile([P, PAGE], U32, name=f"key_pairs{c}")
            nc.vector.tensor_copy(key_pairs[c][:], key_pool[:].bitcast(U32).indirect(list_of(c, c + 1)))

        def score(c):
            key_codes = shared.tile(
                [P, PASSES, PAGE], U16, name=f"key_codes{c}", align_bytes=64, offset=24576 + 2048 * c
            )
            by_pass = key_pairs[c][:].bitcast(U16).rearrange("p (n o) -> p o n", o=PASSES)
            nc.vector.tensor_copy(key_codes[:], by_pass)
            scores[c] = psum.tile([P, PAGE], F32, name=f"scores{c}", tag=f"scores{c}")
            for o in range(PASSES):
                nc.tensor.matmul_mx(
                    out=scores[c][:],
                    lhsT=q_codes[:, o, :].bitcast(FP8X4),
                    lhsT_scale=q_plane[:, o, :],
                    rhs=key_codes[:, o, :].bitcast(FP4X4),
                    rhs_scale=key_planes[:, o * N + c * PAGE : o * N + (c + 1) * PAGE],
                    start=(o == 0),
                    stop=(o == PASSES - 1),
                )

        gather_keys(0)
        for c in range(last):
            gather_keys(c + 1)
            score(c)
        score(last)
        for c in range(last):
            nc.vector.tensor_reduce(maxima[:, c : c + 1], scores[c][:], AX.X, ALU.max, negate=True)
        negated = keep.tile([P, PAGE], F32, name="negated")
        nc.vector.tensor_scalar(
            negated[:], scores[last][:], -1.0, neg_sink[:], ALU.mult, ALU.min, accum_out=maxima[:, last:]
        )

        distance = keep.tile([P, P], F32, name="distance")
        nc.gpsimd.iota(distance[:], [[1, P]], base=0, channel_multiplier=-1, allow_small_or_imprecise_dtypes=True)
        gap = keep.tile([P, P], F32, name="gap")
        nc.scalar.activation(gap[:], distance[:], ACT.Abs)
        ident = keep.tile([P, P], F32, name="ident")
        nc.scalar.activation(ident[:], gap[:], ACT.Relu, bias=1.0, scale=-1.0)
        early_sums = keep.tile([P, 4], F32, name="early_sums")
        sums = keep.tile([P, 2 * PAGES + 1], F32, name="sums")
        turned = {c: psum.tile([P, 4, NQ], F32, name=f"turned{c}", tag=f"turned{c}") for c in (0, 2, 3)}

        def exponential(probs, c, half, bias, row_sum):
            logits, sign = (negated, -1.0) if c == last else (scores[c], 1.0)
            nc.scalar.activation(
                probs,
                logits[:].rearrange("q (s t) -> q s t", t=4)[:, :, 2 * half : 2 * half + 2],
                ACT.Exp,
                bias=bias,
                scale=sign,
                accum_out=row_sum,
            )

        def exponentials(c, half, bias, row_sum):
            probs = shared.tile(
                [P, 2, P], F32, name=f"probs{c}_{half}", align_bytes=64, offset=49152 + 2048 * c + 1024 * half
            )
            exponential(probs[:].rearrange("q t s -> q s t"), c, half, bias, row_sum)
            for t in range(2):
                nc.tensor.transpose(turned[c][:, 2 * half + t, :], probs[:, t, :], ident[:])

        for half in range(2):
            exponentials(0, half, maxima[:, 0:1], early_sums[:, half : half + 1])
        second_probs = keep.tile([P, 2, P, 2], F32, name="second_probs", align_bytes=64)
        for half in range(2):
            exponential(second_probs[:, half, :, :], 1, half, maxima[:, 1:2], early_sums[:, 2 + half : 3 + half])
        spread = psum.tile([P, 4, P], F32, name="spread", tag="scores1")
        for t in range(4):
            nc.tensor.transpose(spread[:, t, :], token_columns[1][:, t : t + 1].to_broadcast([P, P]), ident[:])
        early_scaled = keep.tile([P, 4, NQ], F32, name="early_scaled", align_bytes=64)
        early_back = psum.tile([P, 4, P], F32, name="early_back", tag="scores0")
        for t in range(4):
            nc.scalar.activation(
                early_scaled[:, t, :], turned[0][:, t, :], ACT.Copy, scale=token_columns[0][:, t : t + 1]
            )
            nc.tensor.transpose(early_back[:, t, :], early_scaled[:, t, :], ident[:])

        value_scale_window = value_scale_pool[:].rearrange("p u e -> p (u e)")
        first_plane = shared.tile([P, DV], U8, name="first_plane", align_bytes=64, offset=31744)
        later_planes = shared.tile([P, last * DV], U8, name="later_planes", align_bytes=64, offset=40960)
        value_planes = [first_plane[:]] + [later_planes[:, c * DV : (c + 1) * DV] for c in range(last)]
        neg_max = keep.tile([P, 1], F32, name="neg_max")
        nc.vector.tensor_copy(first_plane[:], value_scale_window.indirect(value_list[:, : DV // 16]))
        nc.vector.tensor_reduce(neg_max[:], maxima[:], AX.X, ALU.min)
        nc.vector.tensor_copy(later_planes[:], value_scale_window.indirect(value_list[:, DV // 16 :]))
        factors = keep.tile([P, 2], F32, name="factors")
        nc.scalar.activation(factors[:], maxima[:, :2], ACT.Exp, bias=neg_max[:], scale=-1.0)
        second_pairs = keep.tile([P, 2, P, 2], BF16, name="second_pairs", align_bytes=64)
        for u in range(2):
            nc.vector.scalar_tensor_tensor(
                second_pairs[:, u, :, :],
                second_probs[:, u, :, :],
                factors[:, 1:2],
                spread[:, 2 * u : 2 * u + 2, :].rearrange("q e s -> q s e"),
                ALU.mult,
                ALU.mult,
            )
        value_codes = shared.tile([P, PAGES * DV], U32, name="value_codes", align_bytes=64, offset=36864)
        nc.vector.tensor_copy(
            value_codes[:], value_pool[:].rearrange("p u e -> p (u e)").bitcast(U32).indirect(value_list[:])
        )

        for half in range(2):
            exponentials(2, half, neg_max[:], sums[:, 4 + half : 5 + half])
        for half in range(2):
            exponentials(last, half, neg_max[:], sums[:, 6 + half : 7 + half])
        second_words = psum.tile([P, 2, NQ], F32, name="second_words", tag="scores2")
        for u in range(2):
            words = second_pairs[:, u, :, :].rearrange("q s e -> q (s e)").bitcast(F32)
            nc.tensor.transpose(second_words[:, u, :], words, ident[:])

        grouped, w_codes, w_plane = {}, {}, {}
        for c in range(PAGES):
            grouped[c] = shared.tile([P, NQ, 4], BF16, name=f"grouped{c}", align_bytes=64, offset=61440 + 1024 * c)

        early_pairs = keep.tile([P, 2, P, 2], BF16, name="early_pairs", align_bytes=64)
        back_pairs = early_back[:].rearrange("q (u e) s -> q u s e", e=2)
        early_words = psum.tile([P, 2, NQ], F32, name="early_words", tag="turned0")
        for u in range(2):
            nc.scalar.activation(early_pairs[:, u, :, :], back_pairs[:, u, :, :], ACT.Copy, scale=factors[:, 0:1])
            words = early_pairs[:, u, :, :].rearrange("q s e -> q (s e)").bitcast(F32)
            nc.tensor.transpose(early_words[:, u, :], words, ident[:])

        def copy_words(c, words):
            nc.scalar.copy(
                grouped[c][:].rearrange("s q t -> s (q t)").bitcast(F32).rearrange("s (q u) -> s q u", u=2),
                words[:].rearrange("s u q -> s q u"),
            )

        copy_words(1, second_words)
        for c in range(2):
            nc.scalar.activation(
                sums[:, 2 * c : 2 * c + 2], early_sums[:, 2 * c : 2 * c + 2], ACT.Copy, scale=factors[:, c : c + 1]
            )
        nc.scalar.activation(sums[:, 2 * PAGES :], sink_col[:], ACT.Exp, bias=neg_max[:])
        total = keep.tile([P, 1], F32, name="total")
        sums_again = keep.tile([P, 2 * PAGES + 1], F32, name="sums_again")
        nc.scalar.activation(sums_again[:], sums[:], ACT.Copy, accum_out=total[:])
        copy_words(0, early_words)

        def weigh(c):
            nc.vector.tensor_tensor(
                grouped[c][:].rearrange("s (g i) t -> s g t i", i=4),
                turned[c][:].rearrange("s t (g i) -> s g t i", i=4),
                token_columns[c][:].unsqueeze(1).unsqueeze(3).to_broadcast([P, NQ // 4, 4, 4]),
                ALU.mult,
            )

        def quantise(c, offset):
            w_codes[c] = shared.tile([P, NQ], U32, name=f"w_codes{c}", align_bytes=64, offset=offset)
            w_plane[c] = shared.tile([P, NQ], U8, name=f"w_plane{c}", align_bytes=64, offset=offset + 512)
            nc.vector.quantize_mx(
                out=w_codes[c][:].bitcast(FP8X4),
                scales=w_plane[c][:],
                in_=grouped[c][:].rearrange("p q t -> p (q t)"),
            )

        weigh(2)
        weigh(last)
        quantise(2, 49152 + 2048 * last + 1024)
        quantise(1, 49152 + 2048 * PAGES - 64)
        quantise(0, 49152)
        quantise(last, 49152 + 2048 * PAGES + 1024)
        inverse = shared.tile([P, 1], F32, name="inverse", offset=61440 + 1024 * last)
        nc.vector.reciprocal(inverse[:], total[:])

        acc = psum.tile([P, DV], F32, name="acc", tag="scores0")
        order = (2, 1, 0, last)
        for c in order:
            nc.tensor.matmul_mx(
                out=acc[:],
                lhsT=w_codes[c][:].bitcast(FP8X4),
                lhsT_scale=w_plane[c][:],
                rhs=value_codes[:, c * DV : (c + 1) * DV].bitcast(FP8X4),
                rhs_scale=value_planes[c],
                start=(c == order[0]),
                stop=(c == order[-1]),
            )

        result = keep.tile([P, DV], F32, name="result")
        nc.vector.tensor_scalar(result[:], acc[:], inverse[:], None, ALU.mult)
        nc.sync.dma_start(out[0], result[:])
